import numpy as np
import ml_dtypes


def mxq(x, axis, fmt="e4m3"):
    dtype, down = {"e4m3": (ml_dtypes.float8_e4m3fn, 7), "e5m2": (ml_dtypes.float8_e5m2, 14)}[fmt]
    v = np.moveaxis(np.asarray(x, np.float32).astype(ml_dtypes.bfloat16).astype(np.float64), axis, -1)
    blocks = v.reshape(v.shape[:-1] + (-1, 32))
    amax = np.abs(blocks).max(-1, keepdims=True)
    byte = np.maximum(np.where(amax > 0, np.frexp(amax)[1] - 1 + 127, 0) - down, 1)
    scale = np.exp2(byte - 127.0)
    codes = (blocks / scale).astype(np.float32).astype(dtype).astype(np.float64)
    return np.moveaxis((codes * scale).reshape(v.shape), -1, axis)


WIDE = False


def mx_kscale(k):
    if not WIDE:
        return np.ones(k)
    levels = np.array([10, -10, 5, -5, 0])
    if k % 512:
        return np.exp2(np.random.permutation(np.resize(levels, k // 32))).repeat(32)
    a = np.empty((k // 512, 16))
    for p in range(k // 512):
        a[p, :8] = np.random.permutation(np.resize(levels, 8))
        for g in range(8):
            far = levels[np.abs(levels - a[p, g]) >= 10]
            a[p, g + 8] = far[np.random.randint(len(far))]
    return np.exp2(a.ravel()).repeat(32)


def f64(x):
    return np.asarray(x).astype(np.float64)


def striped(idx):
    return np.tile(idx.reshape(-1, 16).T, (8, 1)).astype(np.uint16)


def unstriped(offs):
    return offs[:16].T.reshape(-1).astype(np.int64)


def pack_weight(w):
    k, n = w.shape
    w = f64(np.asarray(w, np.float32).astype(ml_dtypes.bfloat16)).reshape(k // 32, 32, n)
    amax = np.abs(w).max(1)
    byte = np.clip(np.where(amax > 0, np.frexp(amax)[1] - 1 + 127 - 7, 1), 1, 254)
    scaled = (w * np.exp2(127.0 - byte)[:, None, :]).reshape(k, n).astype(np.float32)
    words = np.ascontiguousarray(scaled.reshape(k // 512, 128, 4, n).transpose(0, 1, 3, 2)).astype(ml_dtypes.float8_e4m3fn).view(np.uint8)
    return words, np.ascontiguousarray(byte.astype(np.uint8).reshape(k // 512, 16, n))


def unpack_weight(words, scales):
    g, p, n, _ = words.shape
    vals = np.ascontiguousarray(words).view(ml_dtypes.float8_e4m3fn).astype(np.float64) * np.repeat(np.exp2(scales.astype(np.float64) - 127.0), 8, axis=1)[..., None]
    return vals.transpose(0, 1, 3, 2).reshape(g * 512, n)


def gelu(v):
    return 0.5 * v * (1.0 + np.tanh(np.sqrt(2.0 / np.pi) * (v + 0.044715 * v**3)))


K, T, S, N = 512, 4096, 1024, 128
P = 2 ** 7


def setup_inputs():
    n = np.random.standard_normal
    s = mx_kscale(K)[:, None]
    packed_xT = pack_weight(n((K, T)) * s)
    return {
        "x_words": packed_xT[0],
        "x_scales": packed_xT[1],
        "zp": np.tile(np.random.uniform(-0.6, 0.6, T), (P, 1)).astype(np.float32),
        "csum": n((N, 1)).astype(np.float32),
        "w1": (n((K, N)) / np.sqrt(K) / s).astype(np.float32),
        "offs": striped(np.random.permutation(T)[:S]),
    }


def reference(x_words, x_scales, zp, csum, w1, offs):
    xq = unpack_weight(x_words, x_scales)[:, unstriped(offs)]
    y = mxq(f64(w1), 0, "e4m3").T @ xq
    zg = f64(zp)[:1][:, unstriped(offs)]
    return gelu(y - (f64(csum) * zg))

@@ -1,0 +1,110 @@
+from contextlib import ExitStack
+
+import concourse.mybir as mybir
+from concourse.masks import make_identity
+
+K, T, S, N = 512, 4096, 1024, 128
+P = 128
+PACK = 4
+HALF = S // 2
+FLOPS = 2 * K * S * N
+BYTES = K * T + 16 * T + 4 * T + 4 * N + 4 * K * N + 2 * P * S // 16 + 4 * N * S
+
+F32 = mybir.dt.float32
+BF16 = mybir.dt.bfloat16
+I32 = mybir.dt.int32
+U32 = mybir.dt.uint32
+U16 = mybir.dt.uint16
+U8 = mybir.dt.uint8
+FP8X4 = mybir.dt.float8_e4m3fn_x4
+ALU = mybir.AluOpType
+ACT = mybir.ActivationFunctionType
+
+ZROW = P - 1
+PIECES = ((0, 512), (512, 256), (768, 256))
+
+
+def tile_picked_zeropt_gelu_p_kernel(tc, x_words, x_scales, zp, csum, w1, offs, out):
+    nc = tc.nc
+    with ExitStack() as ctx:
+        keep = ctx.enter_context(tc.tile_pool(name="keep", bufs=1))
+        arena = ctx.enter_context(tc.tile_pool(name="arena", bufs=1))
+        psum = ctx.enter_context(tc.psum_pool(name="psum", bufs=1))
+
+        offsets = keep.tile([P, S // 16], U16, name="offsets")
+        words = keep.tile([P, T], I32, name="words", align_bytes=64)
+        scales = arena.tile([P, T], U8, name="scales", align_bytes=64, offset=16384)
+        zwin = arena.tile([P, T], F32, name="zwin", align_bytes=64, offset=0)
+        wraw = arena.tile([P, PACK, N], F32, name="wraw", align_bytes=64, offset=20480)
+        warm = keep.tile([P, 1], F32, name="warm")
+
+        nc.sync.dma_start(offsets[:], offs)
+        nc.sync.dma_start(out=zwin[ZROW:P, :], in_=zp[0:1, :])
+        nc.sync.dma_start(out=wraw[:], in_=w1.rearrange("(p j) n -> p j n", j=PACK))
+        nc.sync.dma_start(out=words[:], in_=x_words[0].rearrange("p n t -> p (n t)").bitcast(I32))
+        nc.vector.memset(scales[:].bitcast(I32), 0)
+        for q in range(4):
+            nc.scalar.dma_start(
+                out=scales[32 * q : 32 * q + 4, :].bitcast(I32),
+                in_=x_scales[0, 4 * q : 4 * q + 4, :].bitcast(I32),
+            )
+        nc.vector.memset(zwin[0:ZROW, :], 0.0)
+        nc.scalar.activation(out=warm[:], in_=wraw[:, 0, 0:1], func=ACT.Gelu_apprx_tanh)
+
+        wgrp = keep.tile([P, N, PACK], BF16, name="wgrp", align_bytes=64)
+        nc.scalar.copy(out=wgrp[:], in_=wraw[:].rearrange("p j n -> p n j"))
+        ident = arena.tile([P, P], F32, name="ident", align_bytes=64, offset=20480)
+        make_identity(nc, ident[:])
+        cs = arena.tile([P, 1], F32, name="cs", align_bytes=64, offset=20992)
+        nc.sync.dma_start(out=cs[:], in_=csum)
+
+        zg = keep.tile([P, S], F32, name="zg")
+        nc.vector.tensor_copy(out=zg[:], in_=zwin[:].indirect(offsets[:]))
+        wq = arena.tile([P, N], U32, name="wq", align_bytes=64, offset=1024)
+        ws = arena.tile([P, N], U8, name="ws", align_bytes=64, offset=1536)
+        nc.vector.quantize_mx(out=wq[:].bitcast(FP8X4), scales=ws[:], in_=wgrp[:].rearrange("p n j -> p (n j)"))
+        sg = arena.tile([P, S], U8, name="sg", align_bytes=64, offset=0)
+        nc.vector.tensor_copy(out=sg[:], in_=scales[:].indirect(offsets[:]))
+
+        zb = []
+        for h in range(2):
+            turned = psum.tile([P, 4, P], F32, name=f"turned{h}")
+            for c in range(4):
+                col = h * HALF + c * P
+                nc.tensor.transpose(turned[:, c, :], zg[:, col : col + P], ident[:])
+            zcol = keep.tile([P, 4], F32, name=f"zcol{h}")
+            nc.scalar.copy(out=zcol[:], in_=turned[:, :, ZROW])
+            spread = psum.tile([P, 4, P], F32, name=f"spread{h}")
+            for c in range(4):
+                nc.tensor.transpose(spread[:, c, :], zcol[:, c : c + 1].to_broadcast([P, P]), ident[:])
+            zrow = keep.tile([P, HALF], F32, name=f"zrow{h}")
+            nc.scalar.copy(out=zrow[:], in_=spread[:].rearrange("p c n -> p (c n)"))
+            zb.append(zrow)
+
+        xg = []
+        for h in range(2):
+            g = arena.tile([P, HALF], U32, name=f"xg{h}", align_bytes=64, offset=16384 + 2048 * h)
+            nc.vector.tensor_copy(
+                out=g[:], in_=words[:].bitcast(U32).indirect(offsets[:, h * HALF // 16 : (h + 1) * HALF // 16])
+            )
+            xg.append(g)
+
+        for c0, width in PIECES:
+            h, lo = divmod(c0, HALF)
+            acc = psum.tile([P, width], F32, name=f"acc{c0}")
+            nc.tensor.matmul_mx(
+                out=acc[:],
+                lhsT=wq[:].bitcast(FP8X4),
+                lhsT_scale=ws[:],
+                rhs=xg[h][:, lo : lo + width].bitcast(FP8X4),
+                rhs_scale=sg[:, c0 : c0 + width],
+                start=True,
+                stop=True,
+            )
+            neg = keep.tile([P, width], F32, name=f"neg{c0}")
+            nc.vector.scalar_tensor_tensor(
+                out=neg[:], in0=zb[h][:, lo : lo + width], scalar=cs[:], in1=acc[:], op0=ALU.mult, op1=ALU.subtract
+            )
+            res = keep.tile([P, width], F32, name=f"res{c0}")
+            nc.scalar.activation(out=res[:], in_=neg[:], func=ACT.Gelu_apprx_tanh, scale=-1.0)
+            nc.sync.dma_start(out=out[:, c0 : c0 + width], in_=res[:])

@@ -48,13 +48,13 @@ def tile_picked_zeropt_gelu_p_kernel(tc, x_words, x_scales, zp, csum, w1, offs, 
                 out=scales[32 * q : 32 * q + 4, :].bitcast(I32),
                 in_=x_scales[0, 4 * q : 4 * q + 4, :].bitcast(I32),
             )
-        nc.vector.memset(zwin[0:ZROW, :], 0.0)
+        nc.vector.memset(zwin[0:ZROW, :].bitcast(I32), 0)
+        ident = keep.tile([P, P], F32, name="ident", align_bytes=64)
+        make_identity(nc, ident[:])
         nc.scalar.activation(out=warm[:], in_=wraw[:, 0, 0:1], func=ACT.Gelu_apprx_tanh)
 
         wgrp = keep.tile([P, N, PACK], BF16, name="wgrp", align_bytes=64)
         nc.scalar.copy(out=wgrp[:], in_=wraw[:].rearrange("p j n -> p n j"))
-        ident = arena.tile([P, P], F32, name="ident", align_bytes=64, offset=20480)
-        make_identity(nc, ident[:])
         cs = arena.tile([P, 1], F32, name="cs", align_bytes=64, offset=20992)
         nc.sync.dma_start(out=cs[:], in_=csum)
 

@@ -1,7 +1,6 @@
 from contextlib import ExitStack
 
 import concourse.mybir as mybir
-from concourse.masks import make_identity
 
 K, T, S, N = 512, 4096, 1024, 128
 P = 128
@@ -22,6 +21,13 @@ ACT = mybir.ActivationFunctionType
 
 ZROW = P - 1
 PIECES = ((0, 512), (512, 256), (768, 256))
+STEP = 256
+
+
+def clear(nc, view, split):
+    nc.vector.memset(view[:, 0 : split - 7], 0)
+    nc.vector.memset(view[:, split - 7 : split], 0)
+    nc.gpsimd.memset(view[:, split:], 0)
 
 
 def tile_picked_zeropt_gelu_p_kernel(tc, x_words, x_scales, zp, csum, w1, offs, out):
@@ -32,46 +38,49 @@ def tile_picked_zeropt_gelu_p_kernel(tc, x_words, x_scales, zp, csum, w1, offs, 
         psum = ctx.enter_context(tc.psum_pool(name="psum", bufs=1))
 
         offsets = keep.tile([P, S // 16], U16, name="offsets")
-        words = keep.tile([P, T], I32, name="words", align_bytes=64)
+        zeros = arena.tile([P, P], F32, name="zeros", align_bytes=64, offset=22528)
         scales = arena.tile([P, T], U8, name="scales", align_bytes=64, offset=16384)
         zwin = arena.tile([P, T], F32, name="zwin", align_bytes=64, offset=0)
         wraw = arena.tile([P, PACK, N], F32, name="wraw", align_bytes=64, offset=20480)
-        warm = keep.tile([P, 1], F32, name="warm")
+        nil = keep.tile([P, 1], F32, name="nil")
+        nc.vector.memset(nil[:], 0.0)
 
         nc.sync.dma_start(offsets[:], offs)
         nc.sync.dma_start(out=zwin[ZROW:P, :], in_=zp[0:1, :])
         nc.sync.dma_start(out=wraw[:], in_=w1.rearrange("(p j) n -> p j n", j=PACK))
-        nc.sync.dma_start(out=words[:], in_=x_words[0].rearrange("p n t -> p (n t)").bitcast(I32))
-        nc.vector.memset(scales[:].bitcast(I32), 0)
-        for q in range(4):
-            nc.scalar.dma_start(
-                out=scales[32 * q : 32 * q + 4, :].bitcast(I32),
-                in_=x_scales[0, 4 * q : 4 * q + 4, :].bitcast(I32),
-            )
-        nc.vector.memset(zwin[0:ZROW, :].bitcast(I32), 0)
         ident = keep.tile([P, P], F32, name="ident", align_bytes=64)
-        make_identity(nc, ident[:])
-        nc.scalar.activation(out=warm[:], in_=wraw[:, 0, 0:1], func=ACT.Gelu_apprx_tanh)
+        nc.gpsimd.memset(zeros[:], 0.0)
+        clear(nc, scales[:].bitcast(I32), 640)
+        for r in range(4):
+            nc.sync.dma_start(out=scales[r:P:32, :].bitcast(I32), in_=x_scales[0, r:16:4, :].bitcast(I32))
+        nc.gpsimd.affine_select(
+            out=ident[:], in_=zeros[:], compare_op=ALU.not_equal, fill=1.0, base=0, pattern=[[-1, P]], channel_multiplier=1
+        )
+        words = arena.tile([P, T], I32, name="words", align_bytes=64, offset=22528)
+        nc.sync.dma_start(out=words[:], in_=x_words[0].rearrange("p n t -> p (n t)").bitcast(I32))
+        clear(nc, zwin[0:ZROW, 0:3112].bitcast(I32), 1480)
+        nc.scalar.activation(
+            out=zwin[0:ZROW, 3112:T], in_=nil[0:ZROW, :].to_broadcast([ZROW, T - 3112]), func=ACT.Gelu_apprx_tanh
+        )
 
         wgrp = keep.tile([P, N, PACK], BF16, name="wgrp", align_bytes=64)
         nc.scalar.copy(out=wgrp[:], in_=wraw[:].rearrange("p j n -> p n j"))
         cs = arena.tile([P, 1], F32, name="cs", align_bytes=64, offset=20992)
         nc.sync.dma_start(out=cs[:], in_=csum)
 
-        zg = keep.tile([P, S], F32, name="zg")
-        nc.vector.tensor_copy(out=zg[:], in_=zwin[:].indirect(offsets[:]))
-        wq = arena.tile([P, N], U32, name="wq", align_bytes=64, offset=1024)
-        ws = arena.tile([P, N], U8, name="ws", align_bytes=64, offset=1536)
-        nc.vector.quantize_mx(out=wq[:].bitcast(FP8X4), scales=ws[:], in_=wgrp[:].rearrange("p n j -> p (n j)"))
-        sg = arena.tile([P, S], U8, name="sg", align_bytes=64, offset=0)
+        zg = []
+        for h in range(2):
+            picked = arena.tile([P, HALF], F32, name=f"zg{h}", align_bytes=64, offset=38912 + 2048 * h)
+            nc.vector.tensor_copy(out=picked[:], in_=zwin[:].indirect(offsets[:, h * HALF // 16 : (h + 1) * HALF // 16]))
+            zg.append(picked)
+        sg = keep.tile([P, S], U8, name="sg", align_bytes=64)
         nc.vector.tensor_copy(out=sg[:], in_=scales[:].indirect(offsets[:]))
 
         zb = []
         for h in range(2):
             turned = psum.tile([P, 4, P], F32, name=f"turned{h}")
             for c in range(4):
-                col = h * HALF + c * P
-                nc.tensor.transpose(turned[:, c, :], zg[:, col : col + P], ident[:])
+                nc.tensor.transpose(turned[:, c, :], zg[h][:, c * P : (c + 1) * P], ident[:])
             zcol = keep.tile([P, 4], F32, name=f"zcol{h}")
             nc.scalar.copy(out=zcol[:], in_=turned[:, :, ZROW])
             spread = psum.tile([P, 4, P], F32, name=f"spread{h}")
@@ -81,9 +90,13 @@ def tile_picked_zeropt_gelu_p_kernel(tc, x_words, x_scales, zp, csum, w1, offs, 
             nc.scalar.copy(out=zrow[:], in_=spread[:].rearrange("p c n -> p (c n)"))
             zb.append(zrow)
 
+        wq = arena.tile([P, N], U32, name="wq", align_bytes=64, offset=38912)
+        ws = keep.tile([P, N], U8, name="ws", align_bytes=64)
+        nc.vector.quantize_mx(out=wq[:].bitcast(FP8X4), scales=ws[:], in_=wgrp[:].rearrange("p n j -> p (n j)"))
+
         xg = []
         for h in range(2):
-            g = arena.tile([P, HALF], U32, name=f"xg{h}", align_bytes=64, offset=16384 + 2048 * h)
+            g = keep.tile([P, HALF], U32, name=f"xg{h}", align_bytes=64)
             nc.vector.tensor_copy(
                 out=g[:], in_=words[:].bitcast(U32).indirect(offsets[:, h * HALF // 16 : (h + 1) * HALF // 16])
             )
@@ -101,10 +114,16 @@ def tile_picked_zeropt_gelu_p_kernel(tc, x_words, x_scales, zp, csum, w1, offs, 
                 start=True,
                 stop=True,
             )
-            neg = keep.tile([P, width], F32, name=f"neg{c0}")
-            nc.vector.scalar_tensor_tensor(
-                out=neg[:], in0=zb[h][:, lo : lo + width], scalar=cs[:], in1=acc[:], op0=ALU.mult, op1=ALU.subtract
-            )
-            res = keep.tile([P, width], F32, name=f"res{c0}")
-            nc.scalar.activation(out=res[:], in_=neg[:], func=ACT.Gelu_apprx_tanh, scale=-1.0)
-            nc.sync.dma_start(out=out[:, c0 : c0 + width], in_=res[:])
+            for e in range(0, width, STEP):
+                neg = keep.tile([P, STEP], F32, name=f"neg{c0 + e}")
+                nc.vector.scalar_tensor_tensor(
+                    out=neg[:],
+                    in0=zb[h][:, lo + e : lo + e + STEP],
+                    scalar=cs[:],
+                    in1=acc[:, e : e + STEP],
+                    op0=ALU.mult,
+                    op1=ALU.subtract,
+                )
+                res = keep.tile([P, STEP], F32, name=f"res{c0 + e}")
+                nc.scalar.activation(out=res[:], in_=neg[:], func=ACT.Gelu_apprx_tanh, scale=-1.0)
+                nc.sync.dma_start(out=out[:, c0 + e : c0 + e + STEP], in_=res[:])

@@ -5,9 +5,13 @@ import concourse.mybir as mybir
 K, T, S, N = 512, 4096, 1024, 128
 P = 128
 PACK = 4
+GROUP = 16
+QUADRANT = 32
+SCALE_ROWS = K // 32
 HALF = S // 2
+CHUNKS = HALF // P
 FLOPS = 2 * K * S * N
-BYTES = K * T + 16 * T + 4 * T + 4 * N + 4 * K * N + 2 * P * S // 16 + 4 * N * S
+BYTES = K * T + SCALE_ROWS * T + 4 * T + 4 * N + 4 * K * N + 2 * P * S // GROUP + 4 * N * S
 
 F32 = mybir.dt.float32
 BF16 = mybir.dt.bfloat16
@@ -19,111 +23,135 @@ FP8X4 = mybir.dt.float8_e4m3fn_x4
 ALU = mybir.AluOpType
 ACT = mybir.ActivationFunctionType
 
-ZROW = P - 1
-PIECES = ((0, 512), (512, 256), (768, 256))
-STEP = 256
+ZP_ROW = P - 1
 
+SCALES_VECTOR_END = 640
+ZP_VECTOR_END = 1696
+ZP_GPSIMD_END = 3288
+ODD_RUN = 7
 
-def clear(nc, view, split):
-    nc.vector.memset(view[:, 0 : split - 7], 0)
-    nc.vector.memset(view[:, split - 7 : split], 0)
-    nc.gpsimd.memset(view[:, split:], 0)
+PRODUCTS = ((0, 512), (512, 128), (640, 256), (896, 128))
+FINISH_WIDTH = 256
+
+AT_ZP_TABLE = 0
+AT_SCALE_TABLE = AT_ZP_TABLE + 4 * T
+AT_WEIGHTS = AT_SCALE_TABLE + T
+AT_WORDS = AT_WEIGHTS + 4 * PACK * N
+AT_PICKED_ZP = AT_WORDS + 4 * T
 
 
 def tile_picked_zeropt_gelu_p_kernel(tc, x_words, x_scales, zp, csum, w1, offs, out):
     nc = tc.nc
     with ExitStack() as ctx:
         keep = ctx.enter_context(tc.tile_pool(name="keep", bufs=1))
-        arena = ctx.enter_context(tc.tile_pool(name="arena", bufs=1))
+        shared = ctx.enter_context(tc.tile_pool(name="shared", bufs=1))
         psum = ctx.enter_context(tc.psum_pool(name="psum", bufs=1))
 
-        offsets = keep.tile([P, S // 16], U16, name="offsets")
-        zeros = arena.tile([P, P], F32, name="zeros", align_bytes=64, offset=22528)
-        scales = arena.tile([P, T], U8, name="scales", align_bytes=64, offset=16384)
-        zwin = arena.tile([P, T], F32, name="zwin", align_bytes=64, offset=0)
-        wraw = arena.tile([P, PACK, N], F32, name="wraw", align_bytes=64, offset=20480)
-        nil = keep.tile([P, 1], F32, name="nil")
-        nc.vector.memset(nil[:], 0.0)
+        offsets = keep.tile([P, S // GROUP], U16, name="offsets")
+        zeros = shared.tile([P, P], F32, name="zeros", align_bytes=64, offset=AT_WORDS)
+        scale_table = shared.tile([P, T], U8, name="scale_table", align_bytes=64, offset=AT_SCALE_TABLE)
+        zp_table = shared.tile([P, T], F32, name="zp_table", align_bytes=64, offset=AT_ZP_TABLE)
+        w_raw = shared.tile([P, PACK, N], F32, name="w_raw", align_bytes=64, offset=AT_WEIGHTS)
+        zp_empty = zp_table[0:ZP_ROW, :]
+        scale_words = scale_table[:].bitcast(I32)
+
+        def half_offsets(h):
+            return offsets[:, h * HALF // GROUP : (h + 1) * HALF // GROUP]
+
+        nc.vector.memset(zp_empty[:, 0:ODD_RUN].bitcast(I32), 0)
 
         nc.sync.dma_start(offsets[:], offs)
-        nc.sync.dma_start(out=zwin[ZROW:P, :], in_=zp[0:1, :])
-        nc.sync.dma_start(out=wraw[:], in_=w1.rearrange("(p j) n -> p j n", j=PACK))
+        nc.sync.dma_start(out=zp_table[ZP_ROW:P, :], in_=zp[0:1, :])
+        nc.sync.dma_start(out=w_raw[:], in_=w1.rearrange("(p j) n -> p j n", j=PACK))
+
         ident = keep.tile([P, P], F32, name="ident", align_bytes=64)
         nc.gpsimd.memset(zeros[:], 0.0)
-        clear(nc, scales[:].bitcast(I32), 640)
-        for r in range(4):
-            nc.sync.dma_start(out=scales[r:P:32, :].bitcast(I32), in_=x_scales[0, r:16:4, :].bitcast(I32))
+        nc.vector.memset(scale_words[:, 0 : SCALES_VECTOR_END - ODD_RUN], 0)
+        nc.vector.memset(scale_words[:, SCALES_VECTOR_END - ODD_RUN : SCALES_VECTOR_END], 0)
+        nc.gpsimd.memset(scale_words[:, SCALES_VECTOR_END:], 0)
+        for r in range(PACK):
+            nc.sync.dma_start(
+                out=scale_table[r:P:QUADRANT, :].bitcast(I32), in_=x_scales[0, r:SCALE_ROWS:PACK, :].bitcast(I32)
+            )
+
         nc.gpsimd.affine_select(
             out=ident[:], in_=zeros[:], compare_op=ALU.not_equal, fill=1.0, base=0, pattern=[[-1, P]], channel_multiplier=1
         )
-        words = arena.tile([P, T], I32, name="words", align_bytes=64, offset=22528)
-        nc.sync.dma_start(out=words[:], in_=x_words[0].rearrange("p n t -> p (n t)").bitcast(I32))
-        clear(nc, zwin[0:ZROW, 0:3112].bitcast(I32), 1480)
+        word_table = shared.tile([P, T], I32, name="word_table", align_bytes=64, offset=AT_WORDS)
+        nc.sync.dma_start(out=word_table[:], in_=x_words[0].rearrange("p n t -> p (n t)").bitcast(I32))
+
+        nc.vector.memset(zp_empty[:, ODD_RUN:ZP_VECTOR_END].bitcast(I32), 0)
+        nc.gpsimd.memset(zp_empty[:, ZP_VECTOR_END:ZP_GPSIMD_END].bitcast(I32), 0)
         nc.scalar.activation(
-            out=zwin[0:ZROW, 3112:T], in_=nil[0:ZROW, :].to_broadcast([ZROW, T - 3112]), func=ACT.Gelu_apprx_tanh
+            out=zp_empty[:, ZP_GPSIMD_END:T],
+            in_=zp_empty[:, 0:1].to_broadcast([ZP_ROW, T - ZP_GPSIMD_END]),
+            func=ACT.Gelu_apprx_tanh,
         )
 
-        wgrp = keep.tile([P, N, PACK], BF16, name="wgrp", align_bytes=64)
-        nc.scalar.copy(out=wgrp[:], in_=wraw[:].rearrange("p j n -> p n j"))
-        cs = arena.tile([P, 1], F32, name="cs", align_bytes=64, offset=20992)
-        nc.sync.dma_start(out=cs[:], in_=csum)
+        w_grouped = keep.tile([P, N, PACK], BF16, name="w_grouped", align_bytes=64)
+        nc.scalar.copy(out=w_grouped[:], in_=w_raw[:].rearrange("p j n -> p n j"))
+        csum_col = shared.tile([P, 1], F32, name="csum_col", align_bytes=64, offset=AT_WEIGHTS)
+        nc.sync.dma_start(out=csum_col[:], in_=csum)
 
-        zg = []
+        zp_picked = []
         for h in range(2):
-            picked = arena.tile([P, HALF], F32, name=f"zg{h}", align_bytes=64, offset=38912 + 2048 * h)
-            nc.vector.tensor_copy(out=picked[:], in_=zwin[:].indirect(offsets[:, h * HALF // 16 : (h + 1) * HALF // 16]))
-            zg.append(picked)
-        sg = keep.tile([P, S], U8, name="sg", align_bytes=64)
-        nc.vector.tensor_copy(out=sg[:], in_=scales[:].indirect(offsets[:]))
-
-        zb = []
-        for h in range(2):
-            turned = psum.tile([P, 4, P], F32, name=f"turned{h}")
-            for c in range(4):
-                nc.tensor.transpose(turned[:, c, :], zg[h][:, c * P : (c + 1) * P], ident[:])
-            zcol = keep.tile([P, 4], F32, name=f"zcol{h}")
-            nc.scalar.copy(out=zcol[:], in_=turned[:, :, ZROW])
-            spread = psum.tile([P, 4, P], F32, name=f"spread{h}")
-            for c in range(4):
-                nc.tensor.transpose(spread[:, c, :], zcol[:, c : c + 1].to_broadcast([P, P]), ident[:])
-            zrow = keep.tile([P, HALF], F32, name=f"zrow{h}")
-            nc.scalar.copy(out=zrow[:], in_=spread[:].rearrange("p c n -> p (c n)"))
-            zb.append(zrow)
-
-        wq = arena.tile([P, N], U32, name="wq", align_bytes=64, offset=38912)
-        ws = keep.tile([P, N], U8, name="ws", align_bytes=64)
-        nc.vector.quantize_mx(out=wq[:].bitcast(FP8X4), scales=ws[:], in_=wgrp[:].rearrange("p n j -> p (n j)"))
-
-        xg = []
-        for h in range(2):
-            g = keep.tile([P, HALF], U32, name=f"xg{h}", align_bytes=64)
-            nc.vector.tensor_copy(
-                out=g[:], in_=words[:].bitcast(U32).indirect(offsets[:, h * HALF // 16 : (h + 1) * HALF // 16])
+            picked = shared.tile(
+                [P, HALF], F32, name=f"zp_picked{h}", align_bytes=64, offset=AT_PICKED_ZP + 4 * HALF * h
             )
-            xg.append(g)
+            nc.vector.tensor_copy(out=picked[:], in_=zp_table[:].indirect(half_offsets(h)))
+            zp_picked.append(picked)
+        x_scale = keep.tile([P, S], U8, name="x_scale", align_bytes=64)
+        nc.vector.tensor_copy(out=x_scale[:], in_=scale_table[:].indirect(offsets[:]))
 
-        for c0, width in PIECES:
-            h, lo = divmod(c0, HALF)
-            acc = psum.tile([P, width], F32, name=f"acc{c0}")
+        zp_spread = []
+        for h in range(2):
+            turned = psum.tile([P, CHUNKS, P], F32, name=f"turned{h}")
+            for c in range(CHUNKS):
+                nc.tensor.transpose(turned[:, c, :], zp_picked[h][:, c * P : (c + 1) * P], ident[:])
+            zp_cols = keep.tile([P, CHUNKS], F32, name=f"zp_cols{h}")
+            nc.scalar.copy(out=zp_cols[:], in_=turned[:, :, ZP_ROW])
+            turned_back = psum.tile([P, CHUNKS, P], F32, name=f"turned_back{h}")
+            for c in range(CHUNKS):
+                nc.tensor.transpose(turned_back[:, c, :], zp_cols[:, c : c + 1].to_broadcast([P, P]), ident[:])
+            spread = keep.tile([P, HALF], F32, name=f"zp_spread{h}")
+            nc.scalar.copy(out=spread[:], in_=turned_back[:].rearrange("p c n -> p (c n)"))
+            zp_spread.append(spread)
+
+        w_codes = shared.tile([P, N], U32, name="w_codes", align_bytes=64, offset=AT_PICKED_ZP)
+        w_scale = keep.tile([P, N], U8, name="w_scale", align_bytes=64)
+        nc.vector.quantize_mx(
+            out=w_codes[:].bitcast(FP8X4), scales=w_scale[:], in_=w_grouped[:].rearrange("p n j -> p (n j)")
+        )
+
+        x_codes = []
+        for h in range(2):
+            codes = keep.tile([P, HALF], U32, name=f"x_codes{h}", align_bytes=64)
+            nc.vector.tensor_copy(out=codes[:], in_=word_table[:].bitcast(U32).indirect(half_offsets(h)))
+            x_codes.append(codes)
+
+        for first, width in PRODUCTS:
+            h, in_half = divmod(first, HALF)
+            acc = psum.tile([P, width], F32, name=f"acc{first}")
             nc.tensor.matmul_mx(
                 out=acc[:],
-                lhsT=wq[:].bitcast(FP8X4),
-                lhsT_scale=ws[:],
-                rhs=xg[h][:, lo : lo + width].bitcast(FP8X4),
-                rhs_scale=sg[:, c0 : c0 + width],
+                lhsT=w_codes[:].bitcast(FP8X4),
+                lhsT_scale=w_scale[:],
+                rhs=x_codes[h][:, in_half : in_half + width].bitcast(FP8X4),
+                rhs_scale=x_scale[:, first : first + width],
                 start=True,
                 stop=True,
             )
-            for e in range(0, width, STEP):
-                neg = keep.tile([P, STEP], F32, name=f"neg{c0 + e}")
+            step = min(FINISH_WIDTH, width)
+            for at in range(0, width, step):
+                negated = keep.tile([P, step], F32, name=f"negated{first + at}")
                 nc.vector.scalar_tensor_tensor(
-                    out=neg[:],
-                    in0=zb[h][:, lo + e : lo + e + STEP],
-                    scalar=cs[:],
-                    in1=acc[:, e : e + STEP],
+                    out=negated[:],
+                    in0=zp_spread[h][:, in_half + at : in_half + at + step],
+                    scalar=csum_col[:],
+                    in1=acc[:, at : at + step],
                     op0=ALU.mult,
                     op1=ALU.subtract,
                 )
-                res = keep.tile([P, STEP], F32, name=f"res{c0 + e}")
-                nc.scalar.activation(out=res[:], in_=neg[:], func=ACT.Gelu_apprx_tanh, scale=-1.0)
-                nc.sync.dma_start(out=out[:, c0 + e : c0 + e + STEP], in_=res[:])
+                result = keep.tile([P, step], F32, name=f"result{first + at}")
+                nc.scalar.activation(out=result[:], in_=negated[:], func=ACT.Gelu_apprx_tanh, scale=-1.0)
+                nc.sync.dma_start(out=out[:, first + at : first + at + step], in_=result[:])

@@ -24,62 +24,46 @@ ALU = mybir.AluOpType
 ACT = mybir.ActivationFunctionType
 
 ZP_ROW = P - 1
+SCALE_END = P // 2
+SCALE_FIRST = SCALE_END - SCALE_ROWS
 
-SCALES_VECTOR_END = 640
-ZP_VECTOR_END = 1696
-ZP_GPSIMD_END = 3288
+ZP_VECTOR_END = 1000
+ZP_GPSIMD_END = 3088
 ODD_RUN = 7
 
-PRODUCTS = ((0, 512), (512, 128), (640, 256), (896, 128))
+PRODUCTS = ((0, 512), (512, 256), (768, 128), (896, 128))
 FINISH_WIDTH = 256
-
-AT_ZP_TABLE = 0
-AT_SCALE_TABLE = AT_ZP_TABLE + 4 * T
-AT_WEIGHTS = AT_SCALE_TABLE + T
-AT_WORDS = AT_WEIGHTS + 4 * PACK * N
-AT_PICKED_ZP = AT_WORDS + 4 * T
 
 
 def tile_picked_zeropt_gelu_p_kernel(tc, x_words, x_scales, zp, csum, w1, offs, out):
     nc = tc.nc
     with ExitStack() as ctx:
         keep = ctx.enter_context(tc.tile_pool(name="keep", bufs=1))
-        shared = ctx.enter_context(tc.tile_pool(name="shared", bufs=1))
         psum = ctx.enter_context(tc.psum_pool(name="psum", bufs=1))
 
         offsets = keep.tile([P, S // GROUP], U16, name="offsets")
-        zeros = shared.tile([P, P], F32, name="zeros", align_bytes=64, offset=AT_WORDS)
-        scale_table = shared.tile([P, T], U8, name="scale_table", align_bytes=64, offset=AT_SCALE_TABLE)
-        zp_table = shared.tile([P, T], F32, name="zp_table", align_bytes=64, offset=AT_ZP_TABLE)
-        w_raw = shared.tile([P, PACK, N], F32, name="w_raw", align_bytes=64, offset=AT_WEIGHTS)
+        scale_table = keep.tile([P, T], U8, name="scale_table", align_bytes=64)
+        zp_table = keep.tile([P, T], F32, name="zp_table", align_bytes=64)
+        w_raw = keep.tile([P, PACK, N], F32, name="w_raw", align_bytes=64)
+        word_table = keep.tile([P, T], I32, name="word_table", align_bytes=64)
+        csum_col = keep.tile([P, 1], F32, name="csum_col", align_bytes=64)
         zp_empty = zp_table[0:ZP_ROW, :]
         scale_words = scale_table[:].bitcast(I32)
 
         def half_offsets(h):
             return offsets[:, h * HALF // GROUP : (h + 1) * HALF // GROUP]
 
-        nc.vector.memset(zp_empty[:, 0:ODD_RUN].bitcast(I32), 0)
-
         nc.sync.dma_start(offsets[:], offs)
+        nc.sync.dma_start(out=scale_words[SCALE_FIRST:SCALE_END, :], in_=x_scales[0].bitcast(I32))
         nc.sync.dma_start(out=zp_table[ZP_ROW:P, :], in_=zp[0:1, :])
         nc.sync.dma_start(out=w_raw[:], in_=w1.rearrange("(p j) n -> p j n", j=PACK))
-
-        ident = keep.tile([P, P], F32, name="ident", align_bytes=64)
-        nc.gpsimd.memset(zeros[:], 0.0)
-        nc.vector.memset(scale_words[:, 0 : SCALES_VECTOR_END - ODD_RUN], 0)
-        nc.vector.memset(scale_words[:, SCALES_VECTOR_END - ODD_RUN : SCALES_VECTOR_END], 0)
-        nc.gpsimd.memset(scale_words[:, SCALES_VECTOR_END:], 0)
-        for r in range(PACK):
-            nc.sync.dma_start(
-                out=scale_table[r:P:QUADRANT, :].bitcast(I32), in_=x_scales[0, r:SCALE_ROWS:PACK, :].bitcast(I32)
-            )
-
-        nc.gpsimd.affine_select(
-            out=ident[:], in_=zeros[:], compare_op=ALU.not_equal, fill=1.0, base=0, pattern=[[-1, P]], channel_multiplier=1
-        )
-        word_table = shared.tile([P, T], I32, name="word_table", align_bytes=64, offset=AT_WORDS)
         nc.sync.dma_start(out=word_table[:], in_=x_words[0].rearrange("p n t -> p (n t)").bitcast(I32))
+        nc.sync.dma_start(out=csum_col[:], in_=csum)
 
+        nc.vector.memset(zp_empty[:, 0:ODD_RUN].bitcast(I32), 0)
+        nc.vector.memset(scale_words[0:SCALE_FIRST, 0 : T // PACK - ODD_RUN], 0)
+        nc.vector.memset(scale_words[0:SCALE_FIRST, T // PACK - ODD_RUN :], 0)
+        nc.gpsimd.memset(scale_words[SCALE_END:P, :], 0)
         nc.vector.memset(zp_empty[:, ODD_RUN:ZP_VECTOR_END].bitcast(I32), 0)
         nc.gpsimd.memset(zp_empty[:, ZP_VECTOR_END:ZP_GPSIMD_END].bitcast(I32), 0)
         nc.scalar.activation(
@@ -88,20 +72,35 @@ def tile_picked_zeropt_gelu_p_kernel(tc, x_words, x_scales, zp, csum, w1, offs, 
             func=ACT.Gelu_apprx_tanh,
         )
 
+        ident = keep.tile([P, P], F32, name="ident", align_bytes=64)
+        nc.gpsimd.memset(ident[:], 0.0)
+        nc.gpsimd.affine_select(
+            out=ident[:], in_=ident[:], compare_op=ALU.not_equal, fill=1.0, base=0, pattern=[[-1, P]], channel_multiplier=1
+        )
+
+        picked_scale = keep.tile([P, S], U8, name="picked_scale", align_bytes=64)
+        nc.vector.tensor_copy(out=picked_scale[:], in_=scale_table[:].indirect(offsets[:]))
+        x_scale = keep.tile([P, S], U8, name="x_scale", align_bytes=64)
+        nc.gpsimd.memset(x_scale[:].bitcast(I32), 0)
+        for q in range(P // QUADRANT):
+            nc.sync.dma_start(
+                out=x_scale[QUADRANT * q : QUADRANT * q + PACK, :].bitcast(I32),
+                in_=picked_scale[SCALE_FIRST + PACK * q : SCALE_FIRST + PACK * (q + 1), :].bitcast(I32),
+            )
+
         w_grouped = keep.tile([P, N, PACK], BF16, name="w_grouped", align_bytes=64)
-        nc.scalar.copy(out=w_grouped[:], in_=w_raw[:].rearrange("p j n -> p n j"))
-        csum_col = shared.tile([P, 1], F32, name="csum_col", align_bytes=64, offset=AT_WEIGHTS)
-        nc.sync.dma_start(out=csum_col[:], in_=csum)
+        nc.vector.tensor_copy(out=w_grouped[:], in_=w_raw[:].rearrange("p j n -> p n j"))
+        w_codes = keep.tile([P, N], U32, name="w_codes", align_bytes=64)
+        w_scale = keep.tile([P, N], U8, name="w_scale", align_bytes=64)
+        nc.vector.quantize_mx(
+            out=w_codes[:].bitcast(FP8X4), scales=w_scale[:], in_=w_grouped[:].rearrange("p n j -> p (n j)")
+        )
 
         zp_picked = []
         for h in range(2):
-            picked = shared.tile(
-                [P, HALF], F32, name=f"zp_picked{h}", align_bytes=64, offset=AT_PICKED_ZP + 4 * HALF * h
-            )
-            nc.vector.tensor_copy(out=picked[:], in_=zp_table[:].indirect(half_offsets(h)))
+            picked = keep.tile([P, HALF], F32, name=f"zp_picked{h}", align_bytes=64)
+            nc.scalar.activation(out=picked[:], in_=zp_table[:].indirect(half_offsets(h)), func=ACT.Copy)
             zp_picked.append(picked)
-        x_scale = keep.tile([P, S], U8, name="x_scale", align_bytes=64)
-        nc.vector.tensor_copy(out=x_scale[:], in_=scale_table[:].indirect(offsets[:]))
 
         zp_spread = []
         for h in range(2):
@@ -116,12 +115,6 @@ def tile_picked_zeropt_gelu_p_kernel(tc, x_words, x_scales, zp, csum, w1, offs, 
             spread = keep.tile([P, HALF], F32, name=f"zp_spread{h}")
             nc.scalar.copy(out=spread[:], in_=turned_back[:].rearrange("p c n -> p (c n)"))
             zp_spread.append(spread)
-
-        w_codes = shared.tile([P, N], U32, name="w_codes", align_bytes=64, offset=AT_PICKED_ZP)
-        w_scale = keep.tile([P, N], U8, name="w_scale", align_bytes=64)
-        nc.vector.quantize_mx(
-            out=w_codes[:].bitcast(FP8X4), scales=w_scale[:], in_=w_grouped[:].rearrange("p n j -> p (n j)")
-        )
 
         x_codes = []
         for h in range(2):

@@ -27,11 +27,11 @@ ZP_ROW = P - 1
 SCALE_END = P // 2
 SCALE_FIRST = SCALE_END - SCALE_ROWS
 
-ZP_VECTOR_END = 1000
-ZP_GPSIMD_END = 3088
+ZP_VECTOR_END = 1256
+ZP_GPSIMD_END = 2984
 ODD_RUN = 7
 
-PRODUCTS = ((0, 512), (512, 256), (768, 128), (896, 128))
+PRODUCTS = ((0, 128), (128, 256), (384, 128), (512, 256), (768, 128), (896, 128))
 FINISH_WIDTH = 256
 
 
@@ -99,12 +99,15 @@ def tile_picked_zeropt_gelu_p_kernel(tc, x_words, x_scales, zp, csum, w1, offs, 
         zp_picked = []
         for h in range(2):
             picked = keep.tile([P, HALF], F32, name=f"zp_picked{h}", align_bytes=64)
-            nc.scalar.activation(out=picked[:], in_=zp_table[:].indirect(half_offsets(h)), func=ACT.Copy)
+            if h == 0:
+                nc.scalar.activation(out=picked[:], in_=zp_table[:].indirect(half_offsets(h)), func=ACT.Copy)
+            else:
+                nc.vector.tensor_copy(out=picked[:], in_=zp_table[:].indirect(half_offsets(h)))
             zp_picked.append(picked)
 
         zp_spread = []
         for h in range(2):
-            turned = psum.tile([P, CHUNKS, P], F32, name=f"turned{h}")
+            turned = psum.tile([P, CHUNKS, P], F32, name=f"turned{h}", tag=f"bank{4 + h}")
             for c in range(CHUNKS):
                 nc.tensor.transpose(turned[:, c, :], zp_picked[h][:, c * P : (c + 1) * P], ident[:])
             zp_cols = keep.tile([P, CHUNKS], F32, name=f"zp_cols{h}")
@@ -124,7 +127,7 @@ def tile_picked_zeropt_gelu_p_kernel(tc, x_words, x_scales, zp, csum, w1, offs, 
 
         for first, width in PRODUCTS:
             h, in_half = divmod(first, HALF)
-            acc = psum.tile([P, width], F32, name=f"acc{first}")
+            acc = psum.tile([P, width], F32, name=f"acc{first}", tag=f"bank{PRODUCTS.index((first, width))}")
             nc.tensor.matmul_mx(
                 out=acc[:],
                 lhsT=w_codes[:].bitcast(FP8X4),

@@ -27,8 +27,8 @@ ZP_ROW = P - 1
 SCALE_END = P // 2
 SCALE_FIRST = SCALE_END - SCALE_ROWS
 
-ZP_VECTOR_END = 1256
-ZP_GPSIMD_END = 2984
+ZP_VECTOR_END = 2104
+ZP_GPSIMD_END = 2504
 ODD_RUN = 7
 
 PRODUCTS = ((0, 128), (128, 256), (384, 128), (512, 256), (768, 128), (896, 128))
@@ -60,6 +60,14 @@ def tile_picked_zeropt_gelu_p_kernel(tc, x_words, x_scales, zp, csum, w1, offs, 
         nc.sync.dma_start(out=word_table[:], in_=x_words[0].rearrange("p n t -> p (n t)").bitcast(I32))
         nc.sync.dma_start(out=csum_col[:], in_=csum)
 
+        ident = keep.tile([P, P], F32, name="ident", align_bytes=64)
+        x_scale = keep.tile([P, S], U8, name="x_scale", align_bytes=64)
+        nc.gpsimd.memset(ident[:], 0.0)
+        nc.gpsimd.memset(x_scale[:].bitcast(I32), 0)
+        nc.gpsimd.affine_select(
+            out=ident[:], in_=ident[:], compare_op=ALU.not_equal, fill=1.0, base=0, pattern=[[-1, P]], channel_multiplier=1
+        )
+
         nc.vector.memset(zp_empty[:, 0:ODD_RUN].bitcast(I32), 0)
         nc.vector.memset(scale_words[0:SCALE_FIRST, 0 : T // PACK - ODD_RUN], 0)
         nc.vector.memset(scale_words[0:SCALE_FIRST, T // PACK - ODD_RUN :], 0)
@@ -72,16 +80,8 @@ def tile_picked_zeropt_gelu_p_kernel(tc, x_words, x_scales, zp, csum, w1, offs, 
             func=ACT.Gelu_apprx_tanh,
         )
 
-        ident = keep.tile([P, P], F32, name="ident", align_bytes=64)
-        nc.gpsimd.memset(ident[:], 0.0)
-        nc.gpsimd.affine_select(
-            out=ident[:], in_=ident[:], compare_op=ALU.not_equal, fill=1.0, base=0, pattern=[[-1, P]], channel_multiplier=1
-        )
-
         picked_scale = keep.tile([P, S], U8, name="picked_scale", align_bytes=64)
         nc.vector.tensor_copy(out=picked_scale[:], in_=scale_table[:].indirect(offsets[:]))
-        x_scale = keep.tile([P, S], U8, name="x_scale", align_bytes=64)
-        nc.gpsimd.memset(x_scale[:].bitcast(I32), 0)
         for q in range(P // QUADRANT):
             nc.sync.dma_start(
                 out=x_scale[QUADRANT * q : QUADRANT * q + PACK, :].bitcast(I32),
@@ -99,10 +99,7 @@ def tile_picked_zeropt_gelu_p_kernel(tc, x_words, x_scales, zp, csum, w1, offs, 
         zp_picked = []
         for h in range(2):
             picked = keep.tile([P, HALF], F32, name=f"zp_picked{h}", align_bytes=64)
-            if h == 0:
-                nc.scalar.activation(out=picked[:], in_=zp_table[:].indirect(half_offsets(h)), func=ACT.Copy)
-            else:
-                nc.vector.tensor_copy(out=picked[:], in_=zp_table[:].indirect(half_offsets(h)))
+            nc.scalar.activation(out=picked[:], in_=zp_table[:].indirect(half_offsets(h)), func=ACT.Copy)
             zp_picked.append(picked)
 
         zp_spread = []

@@ -24,25 +24,27 @@ ALU = mybir.AluOpType
 ACT = mybir.ActivationFunctionType
 
 ZP_ROW = P - 1
-SCALE_END = P // 2
-SCALE_FIRST = SCALE_END - SCALE_ROWS
+SCALE_FIRST = P - SCALE_ROWS
 
-ZP_VECTOR_END = 2104
-ZP_GPSIMD_END = 2504
+ZP_VECTOR_END = 3040
 ODD_RUN = 7
 
 PRODUCTS = ((0, 128), (128, 256), (384, 128), (512, 256), (768, 128), (896, 128))
 FINISH_WIDTH = 256
+
+AT_SCALE_TABLE = 0
+AT_ZEROS = AT_SCALE_TABLE + T
 
 
 def tile_picked_zeropt_gelu_p_kernel(tc, x_words, x_scales, zp, csum, w1, offs, out):
     nc = tc.nc
     with ExitStack() as ctx:
         keep = ctx.enter_context(tc.tile_pool(name="keep", bufs=1))
+        shared = ctx.enter_context(tc.tile_pool(name="shared", bufs=1))
         psum = ctx.enter_context(tc.psum_pool(name="psum", bufs=1))
 
         offsets = keep.tile([P, S // GROUP], U16, name="offsets")
-        scale_table = keep.tile([P, T], U8, name="scale_table", align_bytes=64)
+        scale_table = shared.tile([P, T], U8, name="scale_table", align_bytes=64, offset=AT_SCALE_TABLE)
         zp_table = keep.tile([P, T], F32, name="zp_table", align_bytes=64)
         w_raw = keep.tile([P, PACK, N], F32, name="w_raw", align_bytes=64)
         word_table = keep.tile([P, T], I32, name="word_table", align_bytes=64)
@@ -53,42 +55,47 @@ def tile_picked_zeropt_gelu_p_kernel(tc, x_words, x_scales, zp, csum, w1, offs, 
         def half_offsets(h):
             return offsets[:, h * HALF // GROUP : (h + 1) * HALF // GROUP]
 
+        def clear_beside_gpsimd(words):
+            split = words.shape[1] - ODD_RUN
+            nc.vector.memset(words[:, 0:split], 0)
+            nc.vector.memset(words[:, split:], 0)
+
         nc.sync.dma_start(offsets[:], offs)
-        nc.sync.dma_start(out=scale_words[SCALE_FIRST:SCALE_END, :], in_=x_scales[0].bitcast(I32))
+        nc.sync.dma_start(out=scale_words[SCALE_FIRST:P, :], in_=x_scales[0].bitcast(I32))
         nc.sync.dma_start(out=zp_table[ZP_ROW:P, :], in_=zp[0:1, :])
         nc.sync.dma_start(out=w_raw[:], in_=w1.rearrange("(p j) n -> p j n", j=PACK))
         nc.sync.dma_start(out=word_table[:], in_=x_words[0].rearrange("p n t -> p (n t)").bitcast(I32))
         nc.sync.dma_start(out=csum_col[:], in_=csum)
 
-        ident = keep.tile([P, P], F32, name="ident", align_bytes=64)
+        clear_beside_gpsimd(scale_words[0:SCALE_FIRST, :])
         x_scale = keep.tile([P, S], U8, name="x_scale", align_bytes=64)
-        nc.gpsimd.memset(ident[:], 0.0)
+        ident = keep.tile([P, P], F32, name="ident", align_bytes=64)
+        zeros = shared.tile([P, P], F32, name="zeros", align_bytes=64, offset=AT_ZEROS)
+        nc.gpsimd.memset(zeros[:], 0.0)
         nc.gpsimd.memset(x_scale[:].bitcast(I32), 0)
         nc.gpsimd.affine_select(
-            out=ident[:], in_=ident[:], compare_op=ALU.not_equal, fill=1.0, base=0, pattern=[[-1, P]], channel_multiplier=1
+            out=ident[:], in_=zeros[:], compare_op=ALU.not_equal, fill=1.0, base=0, pattern=[[-1, P]], channel_multiplier=1
         )
 
-        nc.vector.memset(zp_empty[:, 0:ODD_RUN].bitcast(I32), 0)
-        nc.vector.memset(scale_words[0:SCALE_FIRST, 0 : T // PACK - ODD_RUN], 0)
-        nc.vector.memset(scale_words[0:SCALE_FIRST, T // PACK - ODD_RUN :], 0)
-        nc.gpsimd.memset(scale_words[SCALE_END:P, :], 0)
-        nc.vector.memset(zp_empty[:, ODD_RUN:ZP_VECTOR_END].bitcast(I32), 0)
-        nc.gpsimd.memset(zp_empty[:, ZP_VECTOR_END:ZP_GPSIMD_END].bitcast(I32), 0)
+        nc.vector.tensor_copy(
+            out=zp_empty[:, 0:ZP_VECTOR_END], in_=ident[0:ZP_ROW, P - 1 : P].to_broadcast([ZP_ROW, ZP_VECTOR_END])
+        )
         nc.scalar.activation(
-            out=zp_empty[:, ZP_GPSIMD_END:T],
-            in_=zp_empty[:, 0:1].to_broadcast([ZP_ROW, T - ZP_GPSIMD_END]),
+            out=zp_empty[:, ZP_VECTOR_END:T],
+            in_=zeros[0:ZP_ROW, 0:1].to_broadcast([ZP_ROW, T - ZP_VECTOR_END]),
             func=ACT.Gelu_apprx_tanh,
         )
 
-        picked_scale = keep.tile([P, S], U8, name="picked_scale", align_bytes=64)
+        picked_scale = shared.tile([P, S], U8, name="picked_scale", align_bytes=64, offset=AT_ZEROS)
         nc.vector.tensor_copy(out=picked_scale[:], in_=scale_table[:].indirect(offsets[:]))
         for q in range(P // QUADRANT):
+            first_row = SCALE_FIRST + PACK * q
             nc.sync.dma_start(
                 out=x_scale[QUADRANT * q : QUADRANT * q + PACK, :].bitcast(I32),
-                in_=picked_scale[SCALE_FIRST + PACK * q : SCALE_FIRST + PACK * (q + 1), :].bitcast(I32),
+                in_=picked_scale[first_row : first_row + PACK, :].bitcast(I32),
             )
 
-        w_grouped = keep.tile([P, N, PACK], BF16, name="w_grouped", align_bytes=64)
+        w_grouped = shared.tile([P, N, PACK], BF16, name="w_grouped", align_bytes=64, offset=AT_SCALE_TABLE)
         nc.vector.tensor_copy(out=w_grouped[:], in_=w_raw[:].rearrange("p j n -> p n j"))
         w_codes = keep.tile([P, N], U32, name="w_codes", align_bytes=64)
         w_scale = keep.tile([P, N], U8, name="w_scale", align_bytes=64)

@@ -9,7 +9,8 @@ GROUP = 16
 QUADRANT = 32
 SCALE_ROWS = K // 32
 HALF = S // 2
-CHUNKS = HALF // P
+PIECE = 256
+CHUNKS = PIECE // P
 FLOPS = 2 * K * S * N
 BYTES = K * T + SCALE_ROWS * T + 4 * T + 4 * N + 4 * K * N + 2 * P * S // GROUP + 4 * N * S
 
@@ -29,11 +30,13 @@ SCALE_FIRST = P - SCALE_ROWS
 ZP_VECTOR_END = 3040
 ODD_RUN = 7
 
-PRODUCTS = ((0, 128), (128, 256), (384, 128), (512, 256), (768, 128), (896, 128))
-FINISH_WIDTH = 256
+PRODUCTS = ((0, 256), (256, 256), (512, 128), (640, 128), (768, 256))
+FINISH_WIDTH = 128
+STORES = ((0, 256), (256, 256), (512, 256), (768, 128), (896, 128))
 
 AT_SCALE_TABLE = 0
 AT_ZEROS = AT_SCALE_TABLE + T
+AT_WEIGHTS = AT_ZEROS + S
 
 
 def tile_picked_zeropt_gelu_p_kernel(tc, x_words, x_scales, zp, csum, w1, offs, out):
@@ -46,9 +49,8 @@ def tile_picked_zeropt_gelu_p_kernel(tc, x_words, x_scales, zp, csum, w1, offs, 
         offsets = keep.tile([P, S // GROUP], U16, name="offsets")
         scale_table = shared.tile([P, T], U8, name="scale_table", align_bytes=64, offset=AT_SCALE_TABLE)
         zp_table = keep.tile([P, T], F32, name="zp_table", align_bytes=64)
-        w_raw = keep.tile([P, PACK, N], F32, name="w_raw", align_bytes=64)
+        w_raw = shared.tile([P, PACK, N], F32, name="w_raw", align_bytes=64, offset=AT_WEIGHTS)
         word_table = keep.tile([P, T], I32, name="word_table", align_bytes=64)
-        csum_col = keep.tile([P, 1], F32, name="csum_col", align_bytes=64)
         zp_empty = zp_table[0:ZP_ROW, :]
         scale_words = scale_table[:].bitcast(I32)
 
@@ -65,7 +67,6 @@ def tile_picked_zeropt_gelu_p_kernel(tc, x_words, x_scales, zp, csum, w1, offs, 
         nc.sync.dma_start(out=zp_table[ZP_ROW:P, :], in_=zp[0:1, :])
         nc.sync.dma_start(out=w_raw[:], in_=w1.rearrange("(p j) n -> p j n", j=PACK))
         nc.sync.dma_start(out=word_table[:], in_=x_words[0].rearrange("p n t -> p (n t)").bitcast(I32))
-        nc.sync.dma_start(out=csum_col[:], in_=csum)
 
         clear_beside_gpsimd(scale_words[0:SCALE_FIRST, :])
         x_scale = keep.tile([P, S], U8, name="x_scale", align_bytes=64)
@@ -97,31 +98,30 @@ def tile_picked_zeropt_gelu_p_kernel(tc, x_words, x_scales, zp, csum, w1, offs, 
 
         w_grouped = shared.tile([P, N, PACK], BF16, name="w_grouped", align_bytes=64, offset=AT_SCALE_TABLE)
         nc.vector.tensor_copy(out=w_grouped[:], in_=w_raw[:].rearrange("p j n -> p n j"))
+        csum_col = shared.tile([P, 1], F32, name="csum_col", align_bytes=64, offset=AT_WEIGHTS)
+        nc.sync.dma_start(out=csum_col[:], in_=csum)
         w_codes = keep.tile([P, N], U32, name="w_codes", align_bytes=64)
         w_scale = keep.tile([P, N], U8, name="w_scale", align_bytes=64)
         nc.vector.quantize_mx(
             out=w_codes[:].bitcast(FP8X4), scales=w_scale[:], in_=w_grouped[:].rearrange("p n j -> p (n j)")
         )
 
-        zp_picked = []
-        for h in range(2):
-            picked = keep.tile([P, HALF], F32, name=f"zp_picked{h}", align_bytes=64)
-            nc.scalar.activation(out=picked[:], in_=zp_table[:].indirect(half_offsets(h)), func=ACT.Copy)
-            zp_picked.append(picked)
-
-        zp_spread = []
-        for h in range(2):
-            turned = psum.tile([P, CHUNKS, P], F32, name=f"turned{h}", tag=f"bank{4 + h}")
+        zp_spread = keep.tile([P, S], F32, name="zp_spread", align_bytes=64)
+        for i in range(S // PIECE):
+            picked = keep.tile([P, PIECE], F32, name=f"zp_picked{i}", align_bytes=64)
+            piece_offsets = offsets[:, i * PIECE // GROUP : (i + 1) * PIECE // GROUP]
+            nc.scalar.activation(out=picked[:], in_=zp_table[:].indirect(piece_offsets), func=ACT.Copy)
+            turned = psum.tile([P, CHUNKS, P], F32, name=f"turned{i}", tag=f"bank{i}")
             for c in range(CHUNKS):
-                nc.tensor.transpose(turned[:, c, :], zp_picked[h][:, c * P : (c + 1) * P], ident[:])
-            zp_cols = keep.tile([P, CHUNKS], F32, name=f"zp_cols{h}")
+                nc.tensor.transpose(turned[:, c, :], picked[:, c * P : (c + 1) * P], ident[:])
+            zp_cols = keep.tile([P, CHUNKS], F32, name=f"zp_cols{i}")
             nc.scalar.copy(out=zp_cols[:], in_=turned[:, :, ZP_ROW])
-            turned_back = psum.tile([P, CHUNKS, P], F32, name=f"turned_back{h}")
+            turned_back = psum.tile([P, CHUNKS, P], F32, name=f"turned_back{i}", tag=f"bank{S // PIECE + i}")
             for c in range(CHUNKS):
                 nc.tensor.transpose(turned_back[:, c, :], zp_cols[:, c : c + 1].to_broadcast([P, P]), ident[:])
-            spread = keep.tile([P, HALF], F32, name=f"zp_spread{h}")
-            nc.scalar.copy(out=spread[:], in_=turned_back[:].rearrange("p c n -> p (c n)"))
-            zp_spread.append(spread)
+            nc.scalar.copy(
+                out=zp_spread[:, i * PIECE : (i + 1) * PIECE], in_=turned_back[:].rearrange("p c n -> p (c n)")
+            )
 
         x_codes = []
         for h in range(2):
@@ -129,6 +129,8 @@ def tile_picked_zeropt_gelu_p_kernel(tc, x_words, x_scales, zp, csum, w1, offs, 
             nc.vector.tensor_copy(out=codes[:], in_=word_table[:].bitcast(U32).indirect(half_offsets(h)))
             x_codes.append(codes)
 
+        negated = keep.tile([P, S], F32, name="negated", align_bytes=64)
+        result = keep.tile([P, S], F32, name="result", align_bytes=64)
         for first, width in PRODUCTS:
             h, in_half = divmod(first, HALF)
             acc = psum.tile([P, width], F32, name=f"acc{first}", tag=f"bank{PRODUCTS.index((first, width))}")
@@ -141,17 +143,16 @@ def tile_picked_zeropt_gelu_p_kernel(tc, x_words, x_scales, zp, csum, w1, offs, 
                 start=True,
                 stop=True,
             )
-            step = min(FINISH_WIDTH, width)
-            for at in range(0, width, step):
-                negated = keep.tile([P, step], F32, name=f"negated{first + at}")
+            for at in range(0, width, FINISH_WIDTH):
+                cols = slice(first + at, first + at + FINISH_WIDTH)
                 nc.vector.scalar_tensor_tensor(
-                    out=negated[:],
-                    in0=zp_spread[h][:, in_half + at : in_half + at + step],
+                    out=negated[:, cols],
+                    in0=zp_spread[:, cols],
                     scalar=csum_col[:],
-                    in1=acc[:, at : at + step],
+                    in1=acc[:, at : at + FINISH_WIDTH],
                     op0=ALU.mult,
                     op1=ALU.subtract,
                 )
-                result = keep.tile([P, step], F32, name=f"result{first + at}")
-                nc.scalar.activation(out=result[:], in_=negated[:], func=ACT.Gelu_apprx_tanh, scale=-1.0)
-                nc.sync.dma_start(out=out[:, first + at : first + at + step], in_=result[:])
+                nc.scalar.activation(out=result[:, cols], in_=negated[:, cols], func=ACT.Gelu_apprx_tanh, scale=-1.0)
+        for first, width in STORES:
+            nc.sync.dma_start(out=out[:, first : first + width], in_=result[:, first : first + width])

@@ -34,9 +34,10 @@ PRODUCTS = ((0, 256), (256, 256), (512, 128), (640, 128), (768, 256))
 FINISH_WIDTH = 128
 STORES = ((0, 256), (256, 256), (512, 256), (768, 128), (896, 128))
 
-AT_SCALE_TABLE = 0
-AT_ZEROS = AT_SCALE_TABLE + T
-AT_WEIGHTS = AT_ZEROS + S
+AT_PICKED_SCALE = 0
+AT_GROUPED = AT_PICKED_SCALE + S
+AT_ZEROS = AT_GROUPED - 2 * P
+AT_WEIGHTS = AT_GROUPED + 2 * PACK * N
 
 
 def tile_picked_zeropt_gelu_p_kernel(tc, x_words, x_scales, zp, csum, w1, offs, out):
@@ -47,7 +48,7 @@ def tile_picked_zeropt_gelu_p_kernel(tc, x_words, x_scales, zp, csum, w1, offs, 
         psum = ctx.enter_context(tc.psum_pool(name="psum", bufs=1))
 
         offsets = keep.tile([P, S // GROUP], U16, name="offsets")
-        scale_table = shared.tile([P, T], U8, name="scale_table", align_bytes=64, offset=AT_SCALE_TABLE)
+        scale_table = keep.tile([P, T], U8, name="scale_table", align_bytes=64)
         zp_table = keep.tile([P, T], F32, name="zp_table", align_bytes=64)
         w_raw = shared.tile([P, PACK, N], F32, name="w_raw", align_bytes=64, offset=AT_WEIGHTS)
         word_table = keep.tile([P, T], I32, name="word_table", align_bytes=64)
@@ -62,10 +63,10 @@ def tile_picked_zeropt_gelu_p_kernel(tc, x_words, x_scales, zp, csum, w1, offs, 
             nc.vector.memset(words[:, 0:split], 0)
             nc.vector.memset(words[:, split:], 0)
 
+        nc.sync.dma_start(out=w_raw[:], in_=w1.rearrange("(p j) n -> p j n", j=PACK))
         nc.sync.dma_start(offsets[:], offs)
         nc.sync.dma_start(out=scale_words[SCALE_FIRST:P, :], in_=x_scales[0].bitcast(I32))
         nc.sync.dma_start(out=zp_table[ZP_ROW:P, :], in_=zp[0:1, :])
-        nc.sync.dma_start(out=w_raw[:], in_=w1.rearrange("(p j) n -> p j n", j=PACK))
         nc.sync.dma_start(out=word_table[:], in_=x_words[0].rearrange("p n t -> p (n t)").bitcast(I32))
 
         clear_beside_gpsimd(scale_words[0:SCALE_FIRST, :])
@@ -87,7 +88,7 @@ def tile_picked_zeropt_gelu_p_kernel(tc, x_words, x_scales, zp, csum, w1, offs, 
             func=ACT.Gelu_apprx_tanh,
         )
 
-        picked_scale = shared.tile([P, S], U8, name="picked_scale", align_bytes=64, offset=AT_ZEROS)
+        picked_scale = shared.tile([P, S], U8, name="picked_scale", align_bytes=64, offset=AT_PICKED_SCALE)
         nc.vector.tensor_copy(out=picked_scale[:], in_=scale_table[:].indirect(offsets[:]))
         for q in range(P // QUADRANT):
             first_row = SCALE_FIRST + PACK * q
@@ -96,7 +97,7 @@ def tile_picked_zeropt_gelu_p_kernel(tc, x_words, x_scales, zp, csum, w1, offs, 
                 in_=picked_scale[first_row : first_row + PACK, :].bitcast(I32),
             )
 
-        w_grouped = shared.tile([P, N, PACK], BF16, name="w_grouped", align_bytes=64, offset=AT_SCALE_TABLE)
+        w_grouped = shared.tile([P, N, PACK], BF16, name="w_grouped", align_bytes=64, offset=AT_GROUPED)
         nc.vector.tensor_copy(out=w_grouped[:], in_=w_raw[:].rearrange("p j n -> p n j"))
         csum_col = shared.tile([P, 1], F32, name="csum_col", align_bytes=64, offset=AT_WEIGHTS)
         nc.sync.dma_start(out=csum_col[:], in_=csum)

@@ -25,9 +25,12 @@ ALU = mybir.AluOpType
 ACT = mybir.ActivationFunctionType
 
 ZP_ROW = P - 1
-SCALE_FIRST = P - SCALE_ROWS
+SCALE_FIRST = QUADRANT
+SCALE_STEP = 4
+SCALE_END = SCALE_FIRST + SCALE_STEP * SCALE_ROWS
 
-ZP_VECTOR_END = 3040
+SCALES_VECTOR_END = 512
+ZP_VECTOR_END = 2897
 ODD_RUN = 7
 
 PRODUCTS = ((0, 256), (256, 256), (512, 128), (640, 128), (768, 256))
@@ -38,6 +41,7 @@ AT_PICKED_SCALE = 0
 AT_GROUPED = AT_PICKED_SCALE + S
 AT_ZEROS = AT_GROUPED - 2 * P
 AT_WEIGHTS = AT_GROUPED + 2 * PACK * N
+AT_WORDS = AT_WEIGHTS + 4 * PACK * N
 
 
 def tile_picked_zeropt_gelu_p_kernel(tc, x_words, x_scales, zp, csum, w1, offs, out):
@@ -45,13 +49,13 @@ def tile_picked_zeropt_gelu_p_kernel(tc, x_words, x_scales, zp, csum, w1, offs, 
     with ExitStack() as ctx:
         keep = ctx.enter_context(tc.tile_pool(name="keep", bufs=1))
         shared = ctx.enter_context(tc.tile_pool(name="shared", bufs=1))
+        ring = ctx.enter_context(tc.tile_pool(name="ring", bufs=2))
         psum = ctx.enter_context(tc.psum_pool(name="psum", bufs=1))
 
         offsets = keep.tile([P, S // GROUP], U16, name="offsets")
         scale_table = keep.tile([P, T], U8, name="scale_table", align_bytes=64)
         zp_table = keep.tile([P, T], F32, name="zp_table", align_bytes=64)
         w_raw = shared.tile([P, PACK, N], F32, name="w_raw", align_bytes=64, offset=AT_WEIGHTS)
-        word_table = keep.tile([P, T], I32, name="word_table", align_bytes=64)
         zp_empty = zp_table[0:ZP_ROW, :]
         scale_words = scale_table[:].bitcast(I32)
 
@@ -63,24 +67,31 @@ def tile_picked_zeropt_gelu_p_kernel(tc, x_words, x_scales, zp, csum, w1, offs, 
             nc.vector.memset(words[:, 0:split], 0)
             nc.vector.memset(words[:, split:], 0)
 
-        nc.sync.dma_start(out=w_raw[:], in_=w1.rearrange("(p j) n -> p j n", j=PACK))
         nc.sync.dma_start(offsets[:], offs)
-        nc.sync.dma_start(out=scale_words[SCALE_FIRST:P, :], in_=x_scales[0].bitcast(I32))
         nc.sync.dma_start(out=zp_table[ZP_ROW:P, :], in_=zp[0:1, :])
+        nc.sync.dma_start(out=w_raw[:], in_=w1.rearrange("(p j) n -> p j n", j=PACK))
+
+        first_zero = shared.tile([P, 1], F32, name="first_zero", align_bytes=64, offset=AT_WORDS)
+        nc.vector.memset(first_zero[:], 0.0)
+        clear_beside_gpsimd(scale_words[:, 0:SCALES_VECTOR_END])
+        nc.gpsimd.memset(scale_words[:, SCALES_VECTOR_END:], 0)
+        nc.sync.dma_start(out=scale_words[SCALE_FIRST:SCALE_END:SCALE_STEP, :], in_=x_scales[0].bitcast(I32))
+
+        nc.vector.tensor_copy(out=zp_empty[:, 0:1], in_=first_zero[0:ZP_ROW, :])
+        word_table = shared.tile([P, T], I32, name="word_table", align_bytes=64, offset=AT_WORDS)
         nc.sync.dma_start(out=word_table[:], in_=x_words[0].rearrange("p n t -> p (n t)").bitcast(I32))
 
-        clear_beside_gpsimd(scale_words[0:SCALE_FIRST, :])
         x_scale = keep.tile([P, S], U8, name="x_scale", align_bytes=64)
+        clear_beside_gpsimd(x_scale[:].bitcast(I32))
         ident = keep.tile([P, P], F32, name="ident", align_bytes=64)
         zeros = shared.tile([P, P], F32, name="zeros", align_bytes=64, offset=AT_ZEROS)
         nc.gpsimd.memset(zeros[:], 0.0)
-        nc.gpsimd.memset(x_scale[:].bitcast(I32), 0)
         nc.gpsimd.affine_select(
             out=ident[:], in_=zeros[:], compare_op=ALU.not_equal, fill=1.0, base=0, pattern=[[-1, P]], channel_multiplier=1
         )
 
         nc.vector.tensor_copy(
-            out=zp_empty[:, 0:ZP_VECTOR_END], in_=ident[0:ZP_ROW, P - 1 : P].to_broadcast([ZP_ROW, ZP_VECTOR_END])
+            out=zp_empty[:, 1:ZP_VECTOR_END], in_=ident[0:ZP_ROW, P - 1 : P].to_broadcast([ZP_ROW, ZP_VECTOR_END - 1])
         )
         nc.scalar.activation(
             out=zp_empty[:, ZP_VECTOR_END:T],
@@ -91,10 +102,10 @@ def tile_picked_zeropt_gelu_p_kernel(tc, x_words, x_scales, zp, csum, w1, offs, 
         picked_scale = shared.tile([P, S], U8, name="picked_scale", align_bytes=64, offset=AT_PICKED_SCALE)
         nc.vector.tensor_copy(out=picked_scale[:], in_=scale_table[:].indirect(offsets[:]))
         for q in range(P // QUADRANT):
-            first_row = SCALE_FIRST + PACK * q
+            first_row = SCALE_FIRST + SCALE_STEP * PACK * q
             nc.sync.dma_start(
                 out=x_scale[QUADRANT * q : QUADRANT * q + PACK, :].bitcast(I32),
-                in_=picked_scale[first_row : first_row + PACK, :].bitcast(I32),
+                in_=picked_scale[first_row : first_row + SCALE_STEP * PACK : SCALE_STEP, :].bitcast(I32),
             )
 
         w_grouped = shared.tile([P, N, PACK], BF16, name="w_grouped", align_bytes=64, offset=AT_GROUPED)
@@ -109,7 +120,7 @@ def tile_picked_zeropt_gelu_p_kernel(tc, x_words, x_scales, zp, csum, w1, offs, 
 
         zp_spread = keep.tile([P, S], F32, name="zp_spread", align_bytes=64)
         for i in range(S // PIECE):
-            picked = keep.tile([P, PIECE], F32, name=f"zp_picked{i}", align_bytes=64)
+            picked = ring.tile([P, PIECE], F32, name="zp_picked", align_bytes=64)
             piece_offsets = offsets[:, i * PIECE // GROUP : (i + 1) * PIECE // GROUP]
             nc.scalar.activation(out=picked[:], in_=zp_table[:].indirect(piece_offsets), func=ACT.Copy)
             turned = psum.tile([P, CHUNKS, P], F32, name=f"turned{i}", tag=f"bank{i}")

@@ -24,24 +24,22 @@ FP8X4 = mybir.dt.float8_e4m3fn_x4
 ALU = mybir.AluOpType
 ACT = mybir.ActivationFunctionType
 
+EARLY_WORDS = 256
 ZP_ROW = P - 1
 SCALE_FIRST = QUADRANT
 SCALE_STEP = 4
 SCALE_END = SCALE_FIRST + SCALE_STEP * SCALE_ROWS
 
 SCALES_VECTOR_END = 512
-ZP_VECTOR_END = 2897
+ZP_VECTOR_END = 3041
 ODD_RUN = 7
 
 PRODUCTS = ((0, 256), (256, 256), (512, 128), (640, 128), (768, 256))
 FINISH_WIDTH = 128
 STORES = ((0, 256), (256, 256), (512, 256), (768, 128), (896, 128))
 
-AT_PICKED_SCALE = 0
-AT_GROUPED = AT_PICKED_SCALE + S
-AT_ZEROS = AT_GROUPED - 2 * P
-AT_WEIGHTS = AT_GROUPED + 2 * PACK * N
-AT_WORDS = AT_WEIGHTS + 4 * PACK * N
+AT_ZEROS = 0
+AT_WORDS = AT_ZEROS + 2 * PACK * N
 
 
 def tile_picked_zeropt_gelu_p_kernel(tc, x_words, x_scales, zp, csum, w1, offs, out):
@@ -55,7 +53,7 @@ def tile_picked_zeropt_gelu_p_kernel(tc, x_words, x_scales, zp, csum, w1, offs, 
         offsets = keep.tile([P, S // GROUP], U16, name="offsets")
         scale_table = keep.tile([P, T], U8, name="scale_table", align_bytes=64)
         zp_table = keep.tile([P, T], F32, name="zp_table", align_bytes=64)
-        w_raw = shared.tile([P, PACK, N], F32, name="w_raw", align_bytes=64, offset=AT_WEIGHTS)
+        w_raw = keep.tile([P, PACK, N], F32, name="w_raw", align_bytes=64)
         zp_empty = zp_table[0:ZP_ROW, :]
         scale_words = scale_table[:].bitcast(I32)
 
@@ -71,6 +69,13 @@ def tile_picked_zeropt_gelu_p_kernel(tc, x_words, x_scales, zp, csum, w1, offs, 
         nc.sync.dma_start(out=zp_table[ZP_ROW:P, :], in_=zp[0:1, :])
         nc.sync.dma_start(out=w_raw[:], in_=w1.rearrange("(p j) n -> p j n", j=PACK))
 
+        words = x_words[0].rearrange("p n t -> p (n t)").bitcast(I32)
+        early_words = keep.tile([P, EARLY_WORDS], I32, name="early_words", align_bytes=64)
+        nc.sync.dma_start(out=early_words[:], in_=words[:, 0:EARLY_WORDS])
+
+        csum_col = keep.tile([P, 1], F32, name="csum_col", align_bytes=64)
+        nc.sync.dma_start(out=csum_col[:], in_=csum)
+
         first_zero = shared.tile([P, 1], F32, name="first_zero", align_bytes=64, offset=AT_WORDS)
         nc.vector.memset(first_zero[:], 0.0)
         clear_beside_gpsimd(scale_words[:, 0:SCALES_VECTOR_END])
@@ -79,7 +84,7 @@ def tile_picked_zeropt_gelu_p_kernel(tc, x_words, x_scales, zp, csum, w1, offs, 
 
         nc.vector.tensor_copy(out=zp_empty[:, 0:1], in_=first_zero[0:ZP_ROW, :])
         word_table = shared.tile([P, T], I32, name="word_table", align_bytes=64, offset=AT_WORDS)
-        nc.sync.dma_start(out=word_table[:], in_=x_words[0].rearrange("p n t -> p (n t)").bitcast(I32))
+        nc.sync.dma_start(out=word_table[:, EARLY_WORDS:T], in_=words[:, EARLY_WORDS:T])
 
         x_scale = keep.tile([P, S], U8, name="x_scale", align_bytes=64)
         clear_beside_gpsimd(x_scale[:].bitcast(I32))
@@ -91,7 +96,7 @@ def tile_picked_zeropt_gelu_p_kernel(tc, x_words, x_scales, zp, csum, w1, offs, 
         )
 
         nc.vector.tensor_copy(
-            out=zp_empty[:, 1:ZP_VECTOR_END], in_=ident[0:ZP_ROW, P - 1 : P].to_broadcast([ZP_ROW, ZP_VECTOR_END - 1])
+            out=zp_empty[:, 1:ZP_VECTOR_END], in_=zp_empty[:, 0:1].to_broadcast([ZP_ROW, ZP_VECTOR_END - 1])
         )
         nc.scalar.activation(
             out=zp_empty[:, ZP_VECTOR_END:T],
@@ -99,7 +104,7 @@ def tile_picked_zeropt_gelu_p_kernel(tc, x_words, x_scales, zp, csum, w1, offs, 
             func=ACT.Gelu_apprx_tanh,
         )
 
-        picked_scale = shared.tile([P, S], U8, name="picked_scale", align_bytes=64, offset=AT_PICKED_SCALE)
+        picked_scale = keep.tile([P, S], U8, name="picked_scale", align_bytes=64)
         nc.vector.tensor_copy(out=picked_scale[:], in_=scale_table[:].indirect(offsets[:]))
         for q in range(P // QUADRANT):
             first_row = SCALE_FIRST + SCALE_STEP * PACK * q
@@ -108,10 +113,8 @@ def tile_picked_zeropt_gelu_p_kernel(tc, x_words, x_scales, zp, csum, w1, offs, 
                 in_=picked_scale[first_row : first_row + SCALE_STEP * PACK : SCALE_STEP, :].bitcast(I32),
             )
 
-        w_grouped = shared.tile([P, N, PACK], BF16, name="w_grouped", align_bytes=64, offset=AT_GROUPED)
+        w_grouped = shared.tile([P, N, PACK], BF16, name="w_grouped", align_bytes=64, offset=AT_ZEROS)
         nc.vector.tensor_copy(out=w_grouped[:], in_=w_raw[:].rearrange("p j n -> p n j"))
-        csum_col = shared.tile([P, 1], F32, name="csum_col", align_bytes=64, offset=AT_WEIGHTS)
-        nc.sync.dma_start(out=csum_col[:], in_=csum)
         w_codes = keep.tile([P, N], U32, name="w_codes", align_bytes=64)
         w_scale = keep.tile([P, N], U8, name="w_scale", align_bytes=64)
         nc.vector.quantize_mx(
@@ -135,6 +138,7 @@ def tile_picked_zeropt_gelu_p_kernel(tc, x_words, x_scales, zp, csum, w1, offs, 
                 out=zp_spread[:, i * PIECE : (i + 1) * PIECE], in_=turned_back[:].rearrange("p c n -> p (c n)")
             )
 
+        nc.vector.tensor_copy(out=word_table[:, 0:EARLY_WORDS], in_=early_words[:])
         x_codes = []
         for h in range(2):
             codes = keep.tile([P, HALF], U32, name=f"x_codes{h}", align_bytes=64)

@@ -24,14 +24,14 @@ FP8X4 = mybir.dt.float8_e4m3fn_x4
 ALU = mybir.AluOpType
 ACT = mybir.ActivationFunctionType
 
-EARLY_WORDS = 256
+EARLY_WORDS = 896
 ZP_ROW = P - 1
 SCALE_FIRST = QUADRANT
 SCALE_STEP = 4
 SCALE_END = SCALE_FIRST + SCALE_STEP * SCALE_ROWS
 
 SCALES_VECTOR_END = 512
-ZP_VECTOR_END = 3041
+ZP_VECTOR_END = 3329
 ODD_RUN = 7
 
 PRODUCTS = ((0, 256), (256, 256), (512, 128), (640, 128), (768, 256))
@@ -39,7 +39,11 @@ FINISH_WIDTH = 128
 STORES = ((0, 256), (256, 256), (512, 256), (768, 128), (896, 128))
 
 AT_ZEROS = 0
-AT_WORDS = AT_ZEROS + 2 * PACK * N
+AT_SPREAD = AT_ZEROS + S
+AT_SECOND_CODES = AT_SPREAD + 4 * S
+AT_RAW = AT_SECOND_CODES - 2 * PACK * N
+AT_CSUM = AT_SECOND_CODES + 4 * HALF
+AT_WORDS = AT_CSUM + 64
 
 
 def tile_picked_zeropt_gelu_p_kernel(tc, x_words, x_scales, zp, csum, w1, offs, out):
@@ -47,47 +51,39 @@ def tile_picked_zeropt_gelu_p_kernel(tc, x_words, x_scales, zp, csum, w1, offs, 
     with ExitStack() as ctx:
         keep = ctx.enter_context(tc.tile_pool(name="keep", bufs=1))
         shared = ctx.enter_context(tc.tile_pool(name="shared", bufs=1))
-        ring = ctx.enter_context(tc.tile_pool(name="ring", bufs=2))
         psum = ctx.enter_context(tc.psum_pool(name="psum", bufs=1))
 
         offsets = keep.tile([P, S // GROUP], U16, name="offsets")
         scale_table = keep.tile([P, T], U8, name="scale_table", align_bytes=64)
         zp_table = keep.tile([P, T], F32, name="zp_table", align_bytes=64)
-        w_raw = keep.tile([P, PACK, N], F32, name="w_raw", align_bytes=64)
         zp_empty = zp_table[0:ZP_ROW, :]
         scale_words = scale_table[:].bitcast(I32)
 
         def half_offsets(h):
             return offsets[:, h * HALF // GROUP : (h + 1) * HALF // GROUP]
 
-        def clear_beside_gpsimd(words):
-            split = words.shape[1] - ODD_RUN
-            nc.vector.memset(words[:, 0:split], 0)
-            nc.vector.memset(words[:, split:], 0)
-
         nc.sync.dma_start(offsets[:], offs)
         nc.sync.dma_start(out=zp_table[ZP_ROW:P, :], in_=zp[0:1, :])
-        nc.sync.dma_start(out=w_raw[:], in_=w1.rearrange("(p j) n -> p j n", j=PACK))
 
         words = x_words[0].rearrange("p n t -> p (n t)").bitcast(I32)
         early_words = keep.tile([P, EARLY_WORDS], I32, name="early_words", align_bytes=64)
         nc.sync.dma_start(out=early_words[:], in_=words[:, 0:EARLY_WORDS])
 
-        csum_col = keep.tile([P, 1], F32, name="csum_col", align_bytes=64)
-        nc.sync.dma_start(out=csum_col[:], in_=csum)
-
-        first_zero = shared.tile([P, 1], F32, name="first_zero", align_bytes=64, offset=AT_WORDS)
-        nc.vector.memset(first_zero[:], 0.0)
-        clear_beside_gpsimd(scale_words[:, 0:SCALES_VECTOR_END])
+        first_zero = shared.tile([P, HALF + 32], F32, name="first_zero", align_bytes=64, offset=AT_SECOND_CODES)
+        nc.vector.memset(first_zero[:, 0:1], 0.0)
+        nc.vector.memset(scale_words[:, 0 : SCALES_VECTOR_END - ODD_RUN], 0)
+        nc.vector.memset(scale_words[:, SCALES_VECTOR_END - ODD_RUN : SCALES_VECTOR_END], 0)
         nc.gpsimd.memset(scale_words[:, SCALES_VECTOR_END:], 0)
         nc.sync.dma_start(out=scale_words[SCALE_FIRST:SCALE_END:SCALE_STEP, :], in_=x_scales[0].bitcast(I32))
 
-        nc.vector.tensor_copy(out=zp_empty[:, 0:1], in_=first_zero[0:ZP_ROW, :])
+        nc.vector.tensor_copy(out=zp_empty[:, 0:1], in_=first_zero[0:ZP_ROW, 0:1])
         word_table = shared.tile([P, T], I32, name="word_table", align_bytes=64, offset=AT_WORDS)
         nc.sync.dma_start(out=word_table[:, EARLY_WORDS:T], in_=words[:, EARLY_WORDS:T])
+        w_raw = shared.tile([P, PACK, N], F32, name="w_raw", align_bytes=64, offset=AT_RAW)
+        nc.sync.dma_start(out=w_raw[:], in_=w1.rearrange("(p j) n -> p j n", j=PACK))
+        csum_col = shared.tile([P, 1], F32, name="csum_col", align_bytes=64, offset=AT_CSUM)
+        nc.sync.dma_start(out=csum_col[:], in_=csum)
 
-        x_scale = keep.tile([P, S], U8, name="x_scale", align_bytes=64)
-        clear_beside_gpsimd(x_scale[:].bitcast(I32))
         ident = keep.tile([P, P], F32, name="ident", align_bytes=64)
         zeros = shared.tile([P, P], F32, name="zeros", align_bytes=64, offset=AT_ZEROS)
         nc.gpsimd.memset(zeros[:], 0.0)
@@ -106,6 +102,8 @@ def tile_picked_zeropt_gelu_p_kernel(tc, x_words, x_scales, zp, csum, w1, offs, 
 
         picked_scale = keep.tile([P, S], U8, name="picked_scale", align_bytes=64)
         nc.vector.tensor_copy(out=picked_scale[:], in_=scale_table[:].indirect(offsets[:]))
+        x_scale = shared.tile([P, S], U8, name="x_scale", align_bytes=64, offset=AT_ZEROS)
+        nc.vector.memset(x_scale[:].bitcast(I32), 0)
         for q in range(P // QUADRANT):
             first_row = SCALE_FIRST + SCALE_STEP * PACK * q
             nc.sync.dma_start(
@@ -113,43 +111,48 @@ def tile_picked_zeropt_gelu_p_kernel(tc, x_words, x_scales, zp, csum, w1, offs, 
                 in_=picked_scale[first_row : first_row + SCALE_STEP * PACK : SCALE_STEP, :].bitcast(I32),
             )
 
-        w_grouped = shared.tile([P, N, PACK], BF16, name="w_grouped", align_bytes=64, offset=AT_ZEROS)
-        nc.vector.tensor_copy(out=w_grouped[:], in_=w_raw[:].rearrange("p j n -> p n j"))
-        w_codes = keep.tile([P, N], U32, name="w_codes", align_bytes=64)
-        w_scale = keep.tile([P, N], U8, name="w_scale", align_bytes=64)
-        nc.vector.quantize_mx(
-            out=w_codes[:].bitcast(FP8X4), scales=w_scale[:], in_=w_grouped[:].rearrange("p n j -> p (n j)")
-        )
-
-        zp_spread = keep.tile([P, S], F32, name="zp_spread", align_bytes=64)
-        for i in range(S // PIECE):
-            picked = ring.tile([P, PIECE], F32, name="zp_picked", align_bytes=64)
+        pieces = S // PIECE
+        zp_cols = []
+        for i in range(pieces):
+            picked = keep.tile([P, PIECE], F32, name=f"picked{i}", align_bytes=64)
             piece_offsets = offsets[:, i * PIECE // GROUP : (i + 1) * PIECE // GROUP]
             nc.scalar.activation(out=picked[:], in_=zp_table[:].indirect(piece_offsets), func=ACT.Copy)
             turned = psum.tile([P, CHUNKS, P], F32, name=f"turned{i}", tag=f"bank{i}")
             for c in range(CHUNKS):
                 nc.tensor.transpose(turned[:, c, :], picked[:, c * P : (c + 1) * P], ident[:])
-            zp_cols = keep.tile([P, CHUNKS], F32, name=f"zp_cols{i}")
-            nc.scalar.copy(out=zp_cols[:], in_=turned[:, :, ZP_ROW])
-            turned_back = psum.tile([P, CHUNKS, P], F32, name=f"turned_back{i}", tag=f"bank{S // PIECE + i}")
+            cols = keep.tile([P, CHUNKS], F32, name=f"zp_cols{i}")
+            nc.scalar.copy(out=cols[:], in_=turned[:, :, ZP_ROW])
+            zp_cols.append(cols)
+        turned_back = []
+        for i, cols in enumerate(zp_cols):
+            back = psum.tile([P, CHUNKS, P], F32, name=f"turned_back{i}", tag=f"bank{i + 2}")
             for c in range(CHUNKS):
-                nc.tensor.transpose(turned_back[:, c, :], zp_cols[:, c : c + 1].to_broadcast([P, P]), ident[:])
-            nc.scalar.copy(
-                out=zp_spread[:, i * PIECE : (i + 1) * PIECE], in_=turned_back[:].rearrange("p c n -> p (c n)")
-            )
+                nc.tensor.transpose(back[:, c, :], cols[:, c : c + 1].to_broadcast([P, P]), ident[:])
+            turned_back.append(back)
+
+        w_grouped = keep.tile([P, N, PACK], BF16, name="w_grouped", align_bytes=64)
+        nc.scalar.copy(out=w_grouped[:], in_=w_raw[:].rearrange("p j n -> p n j"))
+        zp_spread = shared.tile([P, S], F32, name="zp_spread", align_bytes=64, offset=AT_SPREAD)
+        for i, back in enumerate(turned_back):
+            nc.scalar.copy(out=zp_spread[:, i * PIECE : (i + 1) * PIECE], in_=back[:].rearrange("p c n -> p (c n)"))
 
         nc.vector.tensor_copy(out=word_table[:, 0:EARLY_WORDS], in_=early_words[:])
-        x_codes = []
-        for h in range(2):
-            codes = keep.tile([P, HALF], U32, name=f"x_codes{h}", align_bytes=64)
-            nc.vector.tensor_copy(out=codes[:], in_=word_table[:].bitcast(U32).indirect(half_offsets(h)))
-            x_codes.append(codes)
+        first_codes = keep.tile([P, HALF], U32, name="first_codes", align_bytes=64)
+        nc.vector.tensor_copy(out=first_codes[:], in_=word_table[:].bitcast(U32).indirect(half_offsets(0)))
+        w_codes = keep.tile([P, N], U32, name="w_codes", align_bytes=64)
+        w_scale = keep.tile([P, N], U8, name="w_scale", align_bytes=64)
+        nc.vector.quantize_mx(
+            out=w_codes[:].bitcast(FP8X4), scales=w_scale[:], in_=w_grouped[:].rearrange("p n j -> p (n j)")
+        )
+        second_codes = shared.tile([P, HALF], U32, name="second_codes", align_bytes=64, offset=AT_SECOND_CODES)
+        nc.vector.tensor_copy(out=second_codes[:], in_=word_table[:].bitcast(U32).indirect(half_offsets(1)))
+        x_codes = [first_codes, second_codes]
 
         negated = keep.tile([P, S], F32, name="negated", align_bytes=64)
         result = keep.tile([P, S], F32, name="result", align_bytes=64)
         for first, width in PRODUCTS:
             h, in_half = divmod(first, HALF)
-            acc = psum.tile([P, width], F32, name=f"acc{first}", tag=f"bank{PRODUCTS.index((first, width))}")
+            acc = psum.tile([P, width], F32, name=f"acc{first}", tag=f"bank{(PRODUCTS.index((first, width)) + 6) % 8}")
             nc.tensor.matmul_mx(
                 out=acc[:],
                 lhsT=w_codes[:].bitcast(FP8X4),

@@ -24,23 +24,25 @@ FP8X4 = mybir.dt.float8_e4m3fn_x4
 ALU = mybir.AluOpType
 ACT = mybir.ActivationFunctionType
 
-EARLY_WORDS = 896
+EARLY_WORDS = 768
 ZP_ROW = P - 1
-SCALE_FIRST = QUADRANT
+SCALE_FIRST = QUADRANT - 4
 SCALE_STEP = 4
 SCALE_END = SCALE_FIRST + SCALE_STEP * SCALE_ROWS
 
 SCALES_VECTOR_END = 512
-ZP_VECTOR_END = 3329
+ZP_VECTOR_END = 3041
 ODD_RUN = 7
 
 PRODUCTS = ((0, 256), (256, 256), (512, 128), (640, 128), (768, 256))
 FINISH_WIDTH = 128
 STORES = ((0, 256), (256, 256), (512, 256), (768, 128), (896, 128))
 
-AT_ZEROS = 0
-AT_SPREAD = AT_ZEROS + S
-AT_SECOND_CODES = AT_SPREAD + 4 * S
+LATE_PIECES = 1
+
+AT_SPREAD = 0
+AT_LATE_COLS = AT_SPREAD + 4 * S
+AT_SECOND_CODES = AT_LATE_COLS + 64 * LATE_PIECES
 AT_RAW = AT_SECOND_CODES - 2 * PACK * N
 AT_CSUM = AT_SECOND_CODES + 4 * HALF
 AT_WORDS = AT_CSUM + 64
@@ -62,6 +64,11 @@ def tile_picked_zeropt_gelu_p_kernel(tc, x_words, x_scales, zp, csum, w1, offs, 
         def half_offsets(h):
             return offsets[:, h * HALF // GROUP : (h + 1) * HALF // GROUP]
 
+        def clear_beside_gpsimd(columns):
+            split = columns.shape[1] - ODD_RUN
+            nc.vector.memset(columns[:, 0:split], 0)
+            nc.vector.memset(columns[:, split:], 0)
+
         nc.sync.dma_start(offsets[:], offs)
         nc.sync.dma_start(out=zp_table[ZP_ROW:P, :], in_=zp[0:1, :])
 
@@ -71,8 +78,7 @@ def tile_picked_zeropt_gelu_p_kernel(tc, x_words, x_scales, zp, csum, w1, offs, 
 
         first_zero = shared.tile([P, HALF + 32], F32, name="first_zero", align_bytes=64, offset=AT_SECOND_CODES)
         nc.vector.memset(first_zero[:, 0:1], 0.0)
-        nc.vector.memset(scale_words[:, 0 : SCALES_VECTOR_END - ODD_RUN], 0)
-        nc.vector.memset(scale_words[:, SCALES_VECTOR_END - ODD_RUN : SCALES_VECTOR_END], 0)
+        clear_beside_gpsimd(scale_words[:, 0:SCALES_VECTOR_END])
         nc.gpsimd.memset(scale_words[:, SCALES_VECTOR_END:], 0)
         nc.sync.dma_start(out=scale_words[SCALE_FIRST:SCALE_END:SCALE_STEP, :], in_=x_scales[0].bitcast(I32))
 
@@ -84,8 +90,10 @@ def tile_picked_zeropt_gelu_p_kernel(tc, x_words, x_scales, zp, csum, w1, offs, 
         csum_col = shared.tile([P, 1], F32, name="csum_col", align_bytes=64, offset=AT_CSUM)
         nc.sync.dma_start(out=csum_col[:], in_=csum)
 
+        x_scale = keep.tile([P, S], U8, name="x_scale", align_bytes=64)
+        clear_beside_gpsimd(x_scale[:].bitcast(I32))
         ident = keep.tile([P, P], F32, name="ident", align_bytes=64)
-        zeros = shared.tile([P, P], F32, name="zeros", align_bytes=64, offset=AT_ZEROS)
+        zeros = keep.tile([P, P], F32, name="zeros", align_bytes=64)
         nc.gpsimd.memset(zeros[:], 0.0)
         nc.gpsimd.affine_select(
             out=ident[:], in_=zeros[:], compare_op=ALU.not_equal, fill=1.0, base=0, pattern=[[-1, P]], channel_multiplier=1
@@ -102,8 +110,6 @@ def tile_picked_zeropt_gelu_p_kernel(tc, x_words, x_scales, zp, csum, w1, offs, 
 
         picked_scale = keep.tile([P, S], U8, name="picked_scale", align_bytes=64)
         nc.vector.tensor_copy(out=picked_scale[:], in_=scale_table[:].indirect(offsets[:]))
-        x_scale = shared.tile([P, S], U8, name="x_scale", align_bytes=64, offset=AT_ZEROS)
-        nc.vector.memset(x_scale[:].bitcast(I32), 0)
         for q in range(P // QUADRANT):
             first_row = SCALE_FIRST + SCALE_STEP * PACK * q
             nc.sync.dma_start(
@@ -112,26 +118,34 @@ def tile_picked_zeropt_gelu_p_kernel(tc, x_words, x_scales, zp, csum, w1, offs, 
             )
 
         pieces = S // PIECE
-        zp_cols = []
+        turned = []
         for i in range(pieces):
             picked = keep.tile([P, PIECE], F32, name=f"picked{i}", align_bytes=64)
             piece_offsets = offsets[:, i * PIECE // GROUP : (i + 1) * PIECE // GROUP]
             nc.scalar.activation(out=picked[:], in_=zp_table[:].indirect(piece_offsets), func=ACT.Copy)
-            turned = psum.tile([P, CHUNKS, P], F32, name=f"turned{i}", tag=f"bank{i}")
+            turned.append(psum.tile([P, CHUNKS, P], F32, name=f"turned{i}", tag=f"bank{i}"))
             for c in range(CHUNKS):
-                nc.tensor.transpose(turned[:, c, :], picked[:, c * P : (c + 1) * P], ident[:])
-            cols = keep.tile([P, CHUNKS], F32, name=f"zp_cols{i}")
-            nc.scalar.copy(out=cols[:], in_=turned[:, :, ZP_ROW])
-            zp_cols.append(cols)
-        turned_back = []
-        for i, cols in enumerate(zp_cols):
-            back = psum.tile([P, CHUNKS, P], F32, name=f"turned_back{i}", tag=f"bank{i + 2}")
+                nc.tensor.transpose(turned[i][:, c, :], picked[:, c * P : (c + 1) * P], ident[:])
+
+        def turn_back(i, cols):
+            nc.scalar.copy(out=cols[:], in_=turned[i][:, :, ZP_ROW])
+            back = psum.tile([P, CHUNKS, P], F32, name=f"turned_back{i}", tag=f"bank{pieces + i}")
             for c in range(CHUNKS):
                 nc.tensor.transpose(back[:, c, :], cols[:, c : c + 1].to_broadcast([P, P]), ident[:])
-            turned_back.append(back)
+            return back
+
+        turned_back = []
+        for i in range(pieces - LATE_PIECES):
+            turned_back.append(turn_back(i, keep.tile([P, CHUNKS], F32, name=f"zp_cols{i}")))
 
         w_grouped = keep.tile([P, N, PACK], BF16, name="w_grouped", align_bytes=64)
-        nc.scalar.copy(out=w_grouped[:], in_=w_raw[:].rearrange("p j n -> p n j"))
+        nc.scalar.copy(
+            out=w_grouped[:].rearrange("p (c i) t -> p c t i", i=PACK),
+            in_=w_raw[:].rearrange("p t (c i) -> p c t i", i=PACK),
+        )
+        for j in range(LATE_PIECES):
+            cols = shared.tile([P, CHUNKS], F32, name=f"late_cols{j}", align_bytes=64, offset=AT_LATE_COLS + 64 * j)
+            turned_back.append(turn_back(pieces - LATE_PIECES + j, cols))
         zp_spread = shared.tile([P, S], F32, name="zp_spread", align_bytes=64, offset=AT_SPREAD)
         for i, back in enumerate(turned_back):
             nc.scalar.copy(out=zp_spread[:, i * PIECE : (i + 1) * PIECE], in_=back[:].rearrange("p c n -> p (c n)"))
@@ -152,7 +166,7 @@ def tile_picked_zeropt_gelu_p_kernel(tc, x_words, x_scales, zp, csum, w1, offs, 
         result = keep.tile([P, S], F32, name="result", align_bytes=64)
         for first, width in PRODUCTS:
             h, in_half = divmod(first, HALF)
-            acc = psum.tile([P, width], F32, name=f"acc{first}", tag=f"bank{(PRODUCTS.index((first, width)) + 6) % 8}")
+            acc = psum.tile([P, width], F32, name=f"acc{first}", tag=f"bank{PRODUCTS.index((first, width))}")
             nc.tensor.matmul_mx(
                 out=acc[:],
                 lhsT=w_codes[:].bitcast(FP8X4),

@@ -8,7 +8,8 @@ PACK = 4
 GROUP = 16
 QUADRANT = 32
 SCALE_ROWS = K // 32
-HALF = S // 2
+FIRST = 640
+SECOND = S - FIRST
 PIECE = 256
 CHUNKS = PIECE // P
 FLOPS = 2 * K * S * N
@@ -34,7 +35,7 @@ SCALES_VECTOR_END = 512
 ZP_VECTOR_END = 3041
 ODD_RUN = 7
 
-PRODUCTS = ((0, 256), (256, 256), (512, 128), (640, 128), (768, 256))
+PRODUCTS = ((0, 128), (128, 256), (384, 256), (640, 128), (768, 256))
 FINISH_WIDTH = 128
 STORES = ((0, 256), (256, 256), (512, 256), (768, 128), (896, 128))
 
@@ -44,7 +45,7 @@ AT_SPREAD = 0
 AT_LATE_COLS = AT_SPREAD + 4 * S
 AT_SECOND_CODES = AT_LATE_COLS + 64 * LATE_PIECES
 AT_RAW = AT_SECOND_CODES - 2 * PACK * N
-AT_CSUM = AT_SECOND_CODES + 4 * HALF
+AT_CSUM = AT_SECOND_CODES + 4 * SECOND
 AT_WORDS = AT_CSUM + 64
 
 
@@ -61,9 +62,6 @@ def tile_picked_zeropt_gelu_p_kernel(tc, x_words, x_scales, zp, csum, w1, offs, 
         zp_empty = zp_table[0:ZP_ROW, :]
         scale_words = scale_table[:].bitcast(I32)
 
-        def half_offsets(h):
-            return offsets[:, h * HALF // GROUP : (h + 1) * HALF // GROUP]
-
         def clear_beside_gpsimd(columns):
             split = columns.shape[1] - ODD_RUN
             nc.vector.memset(columns[:, 0:split], 0)
@@ -76,7 +74,7 @@ def tile_picked_zeropt_gelu_p_kernel(tc, x_words, x_scales, zp, csum, w1, offs, 
         early_words = keep.tile([P, EARLY_WORDS], I32, name="early_words", align_bytes=64)
         nc.sync.dma_start(out=early_words[:], in_=words[:, 0:EARLY_WORDS])
 
-        first_zero = shared.tile([P, HALF + 32], F32, name="first_zero", align_bytes=64, offset=AT_SECOND_CODES)
+        first_zero = shared.tile([P, SECOND + 32], F32, name="first_zero", align_bytes=64, offset=AT_SECOND_CODES)
         nc.vector.memset(first_zero[:, 0:1], 0.0)
         clear_beside_gpsimd(scale_words[:, 0:SCALES_VECTOR_END])
         nc.gpsimd.memset(scale_words[:, SCALES_VECTOR_END:], 0)
@@ -151,21 +149,21 @@ def tile_picked_zeropt_gelu_p_kernel(tc, x_words, x_scales, zp, csum, w1, offs, 
             nc.scalar.copy(out=zp_spread[:, i * PIECE : (i + 1) * PIECE], in_=back[:].rearrange("p c n -> p (c n)"))
 
         nc.vector.tensor_copy(out=word_table[:, 0:EARLY_WORDS], in_=early_words[:])
-        first_codes = keep.tile([P, HALF], U32, name="first_codes", align_bytes=64)
-        nc.vector.tensor_copy(out=first_codes[:], in_=word_table[:].bitcast(U32).indirect(half_offsets(0)))
+        first_codes = keep.tile([P, FIRST], U32, name="first_codes", align_bytes=64)
+        nc.vector.tensor_copy(out=first_codes[:], in_=word_table[:].bitcast(U32).indirect(offsets[:, 0 : FIRST // GROUP]))
         w_codes = keep.tile([P, N], U32, name="w_codes", align_bytes=64)
         w_scale = keep.tile([P, N], U8, name="w_scale", align_bytes=64)
         nc.vector.quantize_mx(
             out=w_codes[:].bitcast(FP8X4), scales=w_scale[:], in_=w_grouped[:].rearrange("p n j -> p (n j)")
         )
-        second_codes = shared.tile([P, HALF], U32, name="second_codes", align_bytes=64, offset=AT_SECOND_CODES)
-        nc.vector.tensor_copy(out=second_codes[:], in_=word_table[:].bitcast(U32).indirect(half_offsets(1)))
+        second_codes = shared.tile([P, SECOND], U32, name="second_codes", align_bytes=64, offset=AT_SECOND_CODES)
+        nc.vector.tensor_copy(out=second_codes[:], in_=word_table[:].bitcast(U32).indirect(offsets[:, FIRST // GROUP :]))
         x_codes = [first_codes, second_codes]
 
         negated = keep.tile([P, S], F32, name="negated", align_bytes=64)
         result = keep.tile([P, S], F32, name="result", align_bytes=64)
         for first, width in PRODUCTS:
-            h, in_half = divmod(first, HALF)
+            h, in_half = (0, first) if first < FIRST else (1, first - FIRST)
             acc = psum.tile([P, width], F32, name=f"acc{first}", tag=f"bank{PRODUCTS.index((first, width))}")
             nc.tensor.matmul_mx(
                 out=acc[:],

@@ -10,8 +10,7 @@ QUADRANT = 32
 SCALE_ROWS = K // 32
 FIRST = 640
 SECOND = S - FIRST
-PIECE = 256
-CHUNKS = PIECE // P
+ZP_PIECES = (256, 384, 256, 128)
 FLOPS = 2 * K * S * N
 BYTES = K * T + SCALE_ROWS * T + 4 * T + 4 * N + 4 * K * N + 2 * P * S // GROUP + 4 * N * S
 
@@ -31,19 +30,19 @@ SCALE_FIRST = QUADRANT - 4
 SCALE_STEP = 4
 SCALE_END = SCALE_FIRST + SCALE_STEP * SCALE_ROWS
 
-SCALES_VECTOR_END = 512
+SCALES_VECTOR_END = 448
 ZP_VECTOR_END = 3041
 ODD_RUN = 7
 
-PRODUCTS = ((0, 128), (128, 256), (384, 256), (640, 128), (768, 256))
+BANKS = (((0, 128),), ((128, 256),), ((384, 256),), ((640, 128),), ((768, 256),))
 FINISH_WIDTH = 128
 STORES = ((0, 256), (256, 256), (512, 256), (768, 128), (896, 128))
 
-LATE_PIECES = 1
 
-AT_SPREAD = 0
-AT_LATE_COLS = AT_SPREAD + 4 * S
-AT_SECOND_CODES = AT_LATE_COLS + 64 * LATE_PIECES
+AT_ROUNDED = 0
+AT_SPREAD = AT_ROUNDED + 2 * PACK * N
+AT_LATE_COL = AT_SPREAD + 4 * S
+AT_SECOND_CODES = AT_LATE_COL + 64
 AT_RAW = AT_SECOND_CODES - 2 * PACK * N
 AT_CSUM = AT_SECOND_CODES + 4 * SECOND
 AT_WORDS = AT_CSUM + 64
@@ -76,6 +75,8 @@ def tile_picked_zeropt_gelu_p_kernel(tc, x_words, x_scales, zp, csum, w1, offs, 
 
         first_zero = shared.tile([P, SECOND + 32], F32, name="first_zero", align_bytes=64, offset=AT_SECOND_CODES)
         nc.vector.memset(first_zero[:, 0:1], 0.0)
+        zeros = keep.tile([P, P + 1], F32, name="zeros", align_bytes=64)
+        nc.vector.memset(zeros[:], 0.0)
         clear_beside_gpsimd(scale_words[:, 0:SCALES_VECTOR_END])
         nc.gpsimd.memset(scale_words[:, SCALES_VECTOR_END:], 0)
         nc.sync.dma_start(out=scale_words[SCALE_FIRST:SCALE_END:SCALE_STEP, :], in_=x_scales[0].bitcast(I32))
@@ -88,13 +89,11 @@ def tile_picked_zeropt_gelu_p_kernel(tc, x_words, x_scales, zp, csum, w1, offs, 
         csum_col = shared.tile([P, 1], F32, name="csum_col", align_bytes=64, offset=AT_CSUM)
         nc.sync.dma_start(out=csum_col[:], in_=csum)
 
+        ident = keep.tile([P, P], F32, name="ident", align_bytes=64)
         x_scale = keep.tile([P, S], U8, name="x_scale", align_bytes=64)
         clear_beside_gpsimd(x_scale[:].bitcast(I32))
-        ident = keep.tile([P, P], F32, name="ident", align_bytes=64)
-        zeros = keep.tile([P, P], F32, name="zeros", align_bytes=64)
-        nc.gpsimd.memset(zeros[:], 0.0)
         nc.gpsimd.affine_select(
-            out=ident[:], in_=zeros[:], compare_op=ALU.not_equal, fill=1.0, base=0, pattern=[[-1, P]], channel_multiplier=1
+            out=ident[:], in_=zeros[:, 0:P], compare_op=ALU.not_equal, fill=1.0, base=0, pattern=[[-1, P]], channel_multiplier=1
         )
 
         nc.vector.tensor_copy(
@@ -102,7 +101,7 @@ def tile_picked_zeropt_gelu_p_kernel(tc, x_words, x_scales, zp, csum, w1, offs, 
         )
         nc.scalar.activation(
             out=zp_empty[:, ZP_VECTOR_END:T],
-            in_=zeros[0:ZP_ROW, 0:1].to_broadcast([ZP_ROW, T - ZP_VECTOR_END]),
+            in_=zeros[0:ZP_ROW, P : P + 1].to_broadcast([ZP_ROW, T - ZP_VECTOR_END]),
             func=ACT.Gelu_apprx_tanh,
         )
 
@@ -115,38 +114,41 @@ def tile_picked_zeropt_gelu_p_kernel(tc, x_words, x_scales, zp, csum, w1, offs, 
                 in_=picked_scale[first_row : first_row + SCALE_STEP * PACK : SCALE_STEP, :].bitcast(I32),
             )
 
-        pieces = S // PIECE
+        pieces = len(ZP_PIECES)
+        starts = [sum(ZP_PIECES[:i]) for i in range(pieces + 1)]
         turned = []
-        for i in range(pieces):
-            picked = keep.tile([P, PIECE], F32, name=f"picked{i}", align_bytes=64)
-            piece_offsets = offsets[:, i * PIECE // GROUP : (i + 1) * PIECE // GROUP]
+        for i, width in enumerate(ZP_PIECES):
+            if i == pieces - 2:
+                picked = shared.tile([P, width], F32, name=f"picked{i}", align_bytes=64, offset=AT_ROUNDED)
+            else:
+                picked = keep.tile([P, width], F32, name=f"picked{i}", align_bytes=64)
+            piece_offsets = offsets[:, starts[i] // GROUP : starts[i + 1] // GROUP]
             nc.scalar.activation(out=picked[:], in_=zp_table[:].indirect(piece_offsets), func=ACT.Copy)
-            turned.append(psum.tile([P, CHUNKS, P], F32, name=f"turned{i}", tag=f"bank{i}"))
-            for c in range(CHUNKS):
+            turned.append(psum.tile([P, width // P, P], F32, name=f"turned{i}", tag=f"bank{i}"))
+            for c in range(width // P):
                 nc.tensor.transpose(turned[i][:, c, :], picked[:, c * P : (c + 1) * P], ident[:])
 
-        def turn_back(i, cols):
-            nc.scalar.copy(out=cols[:], in_=turned[i][:, :, ZP_ROW])
-            back = psum.tile([P, CHUNKS, P], F32, name=f"turned_back{i}", tag=f"bank{pieces + i}")
-            for c in range(CHUNKS):
-                nc.tensor.transpose(back[:, c, :], cols[:, c : c + 1].to_broadcast([P, P]), ident[:])
-            return back
-
         turned_back = []
-        for i in range(pieces - LATE_PIECES):
-            turned_back.append(turn_back(i, keep.tile([P, CHUNKS], F32, name=f"zp_cols{i}")))
 
-        w_grouped = keep.tile([P, N, PACK], BF16, name="w_grouped", align_bytes=64)
+        def turn_back(i, zp_cols):
+            chunks = ZP_PIECES[i] // P
+            nc.scalar.copy(out=zp_cols[:], in_=turned[i][:, :, ZP_ROW])
+            turned_back.append(psum.tile([P, chunks, P], F32, name=f"turned_back{i}", tag=f"bank{pieces + i}"))
+            for c in range(chunks):
+                nc.tensor.transpose(turned_back[i][:, c, :], zp_cols[:, c : c + 1].to_broadcast([P, P]), ident[:])
+
+        for i in range(pieces - 1):
+            turn_back(i, keep.tile([P, ZP_PIECES[i] // P], F32, name=f"zp_cols{i}"))
+
+        w_grouped = shared.tile([P, N, PACK], BF16, name="w_grouped", align_bytes=64, offset=AT_ROUNDED)
         nc.scalar.copy(
             out=w_grouped[:].rearrange("p (c i) t -> p c t i", i=PACK),
             in_=w_raw[:].rearrange("p t (c i) -> p c t i", i=PACK),
         )
-        for j in range(LATE_PIECES):
-            cols = shared.tile([P, CHUNKS], F32, name=f"late_cols{j}", align_bytes=64, offset=AT_LATE_COLS + 64 * j)
-            turned_back.append(turn_back(pieces - LATE_PIECES + j, cols))
+        turn_back(pieces - 1, shared.tile([P, 1], F32, name="late_col", align_bytes=64, offset=AT_LATE_COL))
         zp_spread = shared.tile([P, S], F32, name="zp_spread", align_bytes=64, offset=AT_SPREAD)
         for i, back in enumerate(turned_back):
-            nc.scalar.copy(out=zp_spread[:, i * PIECE : (i + 1) * PIECE], in_=back[:].rearrange("p c n -> p (c n)"))
+            nc.scalar.copy(out=zp_spread[:, starts[i] : starts[i + 1]], in_=back[:].rearrange("p c n -> p (c n)"))
 
         nc.vector.tensor_copy(out=word_table[:, 0:EARLY_WORDS], in_=early_words[:])
         first_codes = keep.tile([P, FIRST], U32, name="first_codes", align_bytes=64)
@@ -162,18 +164,21 @@ def tile_picked_zeropt_gelu_p_kernel(tc, x_words, x_scales, zp, csum, w1, offs, 
 
         negated = keep.tile([P, S], F32, name="negated", align_bytes=64)
         result = keep.tile([P, S], F32, name="result", align_bytes=64)
-        for first, width in PRODUCTS:
-            h, in_half = (0, first) if first < FIRST else (1, first - FIRST)
-            acc = psum.tile([P, width], F32, name=f"acc{first}", tag=f"bank{PRODUCTS.index((first, width))}")
-            nc.tensor.matmul_mx(
-                out=acc[:],
-                lhsT=w_codes[:].bitcast(FP8X4),
-                lhsT_scale=w_scale[:],
-                rhs=x_codes[h][:, in_half : in_half + width].bitcast(FP8X4),
-                rhs_scale=x_scale[:, first : first + width],
-                start=True,
-                stop=True,
-            )
+        for b, products in enumerate(BANKS):
+            first = products[0][0]
+            width = sum(n for start, n in products)
+            acc = psum.tile([P, width], F32, name=f"acc{first}", tag=f"bank{b}")
+            for start, n in products:
+                h, in_half = (0, start) if start < FIRST else (1, start - FIRST)
+                nc.tensor.matmul_mx(
+                    out=acc[:, start - first : start - first + n],
+                    lhsT=w_codes[:].bitcast(FP8X4),
+                    lhsT_scale=w_scale[:],
+                    rhs=x_codes[h][:, in_half : in_half + n].bitcast(FP8X4),
+                    rhs_scale=x_scale[:, start : start + n],
+                    start=True,
+                    stop=True,
+                )
             for at in range(0, width, FINISH_WIDTH):
                 cols = slice(first + at, first + at + FINISH_WIDTH)
                 nc.vector.scalar_tensor_tensor(

@@ -36,7 +36,7 @@ ODD_RUN = 7
 
 BANKS = (((0, 128),), ((128, 256),), ((384, 256),), ((640, 128),), ((768, 256),))
 FINISH_WIDTH = 128
-STORES = ((0, 256), (256, 256), (512, 256), (768, 128), (896, 128))
+STORES = ((0, 128), (128, 128), (256, 256), (512, 256), (768, 256))
 
 
 AT_ROUNDED = 0

@@ -31,7 +31,8 @@ SCALE_STEP = 4
 SCALE_END = SCALE_FIRST + SCALE_STEP * SCALE_ROWS
 
 SCALES_VECTOR_END = 448
-ZP_VECTOR_END = 3041
+ZP_BESIDE_END = 302
+ZP_VECTOR_END = 3170
 ODD_RUN = 7
 
 BANKS = (((0, 128),), ((128, 256),), ((384, 256),), ((640, 128),), ((768, 256),))
@@ -90,15 +91,17 @@ def tile_picked_zeropt_gelu_p_kernel(tc, x_words, x_scales, zp, csum, w1, offs, 
         nc.sync.dma_start(out=csum_col[:], in_=csum)
 
         ident = keep.tile([P, P], F32, name="ident", align_bytes=64)
-        x_scale = keep.tile([P, S], U8, name="x_scale", align_bytes=64)
-        clear_beside_gpsimd(x_scale[:].bitcast(I32))
         nc.gpsimd.affine_select(
             out=ident[:], in_=zeros[:, 0:P], compare_op=ALU.not_equal, fill=1.0, base=0, pattern=[[-1, P]], channel_multiplier=1
         )
 
+        nc.vector.memset(zp_empty[:, 1:ZP_BESIDE_END], 0.0)
         nc.vector.tensor_copy(
-            out=zp_empty[:, 1:ZP_VECTOR_END], in_=zp_empty[:, 0:1].to_broadcast([ZP_ROW, ZP_VECTOR_END - 1])
+            out=zp_empty[:, ZP_BESIDE_END:ZP_VECTOR_END],
+            in_=zp_empty[:, 0:1].to_broadcast([ZP_ROW, ZP_VECTOR_END - ZP_BESIDE_END]),
         )
+        x_scale = keep.tile([P, S], U8, name="x_scale", align_bytes=64)
+        nc.vector.memset(x_scale[:].bitcast(I32), 0)
         nc.scalar.activation(
             out=zp_empty[:, ZP_VECTOR_END:T],
             in_=zeros[0:ZP_ROW, P : P + 1].to_broadcast([ZP_ROW, T - ZP_VECTOR_END]),
@@ -167,7 +170,7 @@ def tile_picked_zeropt_gelu_p_kernel(tc, x_words, x_scales, zp, csum, w1, offs, 
         for b, products in enumerate(BANKS):
             first = products[0][0]
             width = sum(n for start, n in products)
-            acc = psum.tile([P, width], F32, name=f"acc{first}", tag=f"bank{b}")
+            acc = psum.tile([P, width], F32, name=f"acc{first}", tag=f"bank{b if first < FIRST else b + 3}")
             for start, n in products:
                 h, in_half = (0, start) if start < FIRST else (1, start - FIRST)
                 nc.tensor.matmul_mx(

@@ -10,7 +10,7 @@ QUADRANT = 32
 SCALE_ROWS = K // 32
 FIRST = 640
 SECOND = S - FIRST
-ZP_PIECES = (256, 384, 256, 128)
+ZP_PIECES = (512, 128, 256, 128)
 FLOPS = 2 * K * S * N
 BYTES = K * T + SCALE_ROWS * T + 4 * T + 4 * N + 4 * K * N + 2 * P * S // GROUP + 4 * N * S
 
@@ -35,7 +35,7 @@ ZP_BESIDE_END = 302
 ZP_VECTOR_END = 3170
 ODD_RUN = 7
 
-BANKS = (((0, 128),), ((128, 256),), ((384, 256),), ((640, 128),), ((768, 256),))
+PRODUCTS = ((0, 128, 0), (128, 128, 1), (256, 128, 2), (384, 128, 3), (512, 128, 5), (640, 128, 6), (768, 256, 7))
 FINISH_WIDTH = 128
 STORES = ((0, 128), (128, 128), (256, 256), (512, 256), (768, 256))
 
@@ -167,21 +167,18 @@ def tile_picked_zeropt_gelu_p_kernel(tc, x_words, x_scales, zp, csum, w1, offs, 
 
         negated = keep.tile([P, S], F32, name="negated", align_bytes=64)
         result = keep.tile([P, S], F32, name="result", align_bytes=64)
-        for b, products in enumerate(BANKS):
-            first = products[0][0]
-            width = sum(n for start, n in products)
-            acc = psum.tile([P, width], F32, name=f"acc{first}", tag=f"bank{b if first < FIRST else b + 3}")
-            for start, n in products:
-                h, in_half = (0, start) if start < FIRST else (1, start - FIRST)
-                nc.tensor.matmul_mx(
-                    out=acc[:, start - first : start - first + n],
-                    lhsT=w_codes[:].bitcast(FP8X4),
-                    lhsT_scale=w_scale[:],
-                    rhs=x_codes[h][:, in_half : in_half + n].bitcast(FP8X4),
-                    rhs_scale=x_scale[:, start : start + n],
-                    start=True,
-                    stop=True,
-                )
+        for first, width, b in PRODUCTS:
+            h, in_half = (0, first) if first < FIRST else (1, first - FIRST)
+            acc = psum.tile([P, width], F32, name=f"acc{first}", tag=f"bank{b}")
+            nc.tensor.matmul_mx(
+                out=acc[:],
+                lhsT=w_codes[:].bitcast(FP8X4),
+                lhsT_scale=w_scale[:],
+                rhs=x_codes[h][:, in_half : in_half + width].bitcast(FP8X4),
+                rhs_scale=x_scale[:, first : first + width],
+                start=True,
+                stop=True,
+            )
             for at in range(0, width, FINISH_WIDTH):
                 cols = slice(first + at, first + at + FINISH_WIDTH)
                 nc.vector.scalar_tensor_tensor(

from contextlib import ExitStack

import concourse.mybir as mybir

K, T, S, N = 512, 4096, 1024, 128
P = 128
PACK = 4
GROUP = 16
QUADRANT = 32
SCALE_ROWS = K // 32
FIRST = 640
SECOND = S - FIRST
ZP_PIECES = (512, 128, 256, 128)
FLOPS = 2 * K * S * N
BYTES = K * T + SCALE_ROWS * T + 4 * T + 4 * N + 4 * K * N + 2 * P * S // GROUP + 4 * N * S

F32 = mybir.dt.float32
BF16 = mybir.dt.bfloat16
I32 = mybir.dt.int32
U32 = mybir.dt.uint32
U16 = mybir.dt.uint16
U8 = mybir.dt.uint8
FP8X4 = mybir.dt.float8_e4m3fn_x4
ALU = mybir.AluOpType
ACT = mybir.ActivationFunctionType

EARLY_WORDS = 768
ZP_ROW = P - 1
SCALE_FIRST = QUADRANT - 4
SCALE_STEP = 4
SCALE_END = SCALE_FIRST + SCALE_STEP * SCALE_ROWS

SCALES_VECTOR_END = 448
ZP_BESIDE_END = 302
ZP_VECTOR_END = 3170
ODD_RUN = 7

PRODUCTS = ((0, 128, 0), (128, 128, 1), (256, 128, 2), (384, 128, 3), (512, 128, 5), (640, 128, 6), (768, 256, 7))
FINISH_WIDTH = 128
STORES = ((0, 128), (128, 128), (256, 256), (512, 256), (768, 256))


AT_ROUNDED = 0
AT_SPREAD = AT_ROUNDED + 2 * PACK * N
AT_LATE_COL = AT_SPREAD + 4 * S
AT_SECOND_CODES = AT_LATE_COL + 64
AT_RAW = AT_SECOND_CODES - 2 * PACK * N
AT_CSUM = AT_SECOND_CODES + 4 * SECOND
AT_WORDS = AT_CSUM + 64


def tile_picked_zeropt_gelu_p_kernel(tc, x_words, x_scales, zp, csum, w1, offs, out):
    nc = tc.nc
    with ExitStack() as ctx:
        keep = ctx.enter_context(tc.tile_pool(name="keep", bufs=1))
        shared = ctx.enter_context(tc.tile_pool(name="shared", bufs=1))
        psum = ctx.enter_context(tc.psum_pool(name="psum", bufs=1))

        offsets = keep.tile([P, S // GROUP], U16, name="offsets")
        scale_table = keep.tile([P, T], U8, name="scale_table", align_bytes=64)
        zp_table = keep.tile([P, T], F32, name="zp_table", align_bytes=64)
        zp_empty = zp_table[0:ZP_ROW, :]
        scale_words = scale_table[:].bitcast(I32)

        def clear_beside_gpsimd(columns):
            split = columns.shape[1] - ODD_RUN
            nc.vector.memset(columns[:, 0:split], 0)
            nc.vector.memset(columns[:, split:], 0)

        nc.sync.dma_start(offsets[:], offs)
        nc.sync.dma_start(out=zp_table[ZP_ROW:P, :], in_=zp[0:1, :])

        words = x_words[0].rearrange("p n t -> p (n t)").bitcast(I32)
        early_words = keep.tile([P, EARLY_WORDS], I32, name="early_words", align_bytes=64)
        nc.sync.dma_start(out=early_words[:], in_=words[:, 0:EARLY_WORDS])

        first_zero = shared.tile([P, SECOND + 32], F32, name="first_zero", align_bytes=64, offset=AT_SECOND_CODES)
        nc.vector.memset(first_zero[:, 0:1], 0.0)
        zeros = keep.tile([P, P + 1], F32, name="zeros", align_bytes=64)
        nc.vector.memset(zeros[:], 0.0)
        clear_beside_gpsimd(scale_words[:, 0:SCALES_VECTOR_END])
        nc.gpsimd.memset(scale_words[:, SCALES_VECTOR_END:], 0)
        nc.sync.dma_start(out=scale_words[SCALE_FIRST:SCALE_END:SCALE_STEP, :], in_=x_scales[0].bitcast(I32))

        nc.vector.tensor_copy(out=zp_empty[:, 0:1], in_=first_zero[0:ZP_ROW, 0:1])
        word_table = shared.tile([P, T], I32, name="word_table", align_bytes=64, offset=AT_WORDS)
        nc.sync.dma_start(out=word_table[:, EARLY_WORDS:T], in_=words[:, EARLY_WORDS:T])
        w_raw = shared.tile([P, PACK, N], F32, name="w_raw", align_bytes=64, offset=AT_RAW)
        nc.sync.dma_start(out=w_raw[:], in_=w1.rearrange("(p j) n -> p j n", j=PACK))
        csum_col = shared.tile([P, 1], F32, name="csum_col", align_bytes=64, offset=AT_CSUM)
        nc.sync.dma_start(out=csum_col[:], in_=csum)

        ident = keep.tile([P, P], F32, name="ident", align_bytes=64)
        nc.gpsimd.affine_select(
            out=ident[:], in_=zeros[:, 0:P], compare_op=ALU.not_equal, fill=1.0, base=0, pattern=[[-1, P]], channel_multiplier=1
        )

        nc.vector.memset(zp_empty[:, 1:ZP_BESIDE_END], 0.0)
        nc.vector.tensor_copy(
            out=zp_empty[:, ZP_BESIDE_END:ZP_VECTOR_END],
            in_=zp_empty[:, 0:1].to_broadcast([ZP_ROW, ZP_VECTOR_END - ZP_BESIDE_END]),
        )
        x_scale = keep.tile([P, S], U8, name="x_scale", align_bytes=64)
        nc.vector.memset(x_scale[:].bitcast(I32), 0)
        nc.scalar.activation(
            out=zp_empty[:, ZP_VECTOR_END:T],
            in_=zeros[0:ZP_ROW, P : P + 1].to_broadcast([ZP_ROW, T - ZP_VECTOR_END]),
            func=ACT.Gelu_apprx_tanh,
        )

        picked_scale = keep.tile([P, S], U8, name="picked_scale", align_bytes=64)
        nc.vector.tensor_copy(out=picked_scale[:], in_=scale_table[:].indirect(offsets[:]))
        for q in range(P // QUADRANT):
            first_row = SCALE_FIRST + SCALE_STEP * PACK * q
            nc.sync.dma_start(
                out=x_scale[QUADRANT * q : QUADRANT * q + PACK, :].bitcast(I32),
                in_=picked_scale[first_row : first_row + SCALE_STEP * PACK : SCALE_STEP, :].bitcast(I32),
            )

        pieces = len(ZP_PIECES)
        starts = [sum(ZP_PIECES[:i]) for i in range(pieces + 1)]
        turned = []
        for i, width in enumerate(ZP_PIECES):
            if i == pieces - 2:
                picked = shared.tile([P, width], F32, name=f"picked{i}", align_bytes=64, offset=AT_ROUNDED)
            else:
                picked = keep.tile([P, width], F32, name=f"picked{i}", align_bytes=64)
            piece_offsets = offsets[:, starts[i] // GROUP : starts[i + 1] // GROUP]
            nc.scalar.activation(out=picked[:], in_=zp_table[:].indirect(piece_offsets), func=ACT.Copy)
            turned.append(psum.tile([P, width // P, P], F32, name=f"turned{i}", tag=f"bank{i}"))
            for c in range(width // P):
                nc.tensor.transpose(turned[i][:, c, :], picked[:, c * P : (c + 1) * P], ident[:])

        turned_back = []

        def turn_back(i, zp_cols):
            chunks = ZP_PIECES[i] // P
            nc.scalar.copy(out=zp_cols[:], in_=turned[i][:, :, ZP_ROW])
            turned_back.append(psum.tile([P, chunks, P], F32, name=f"turned_back{i}", tag=f"bank{pieces + i}"))
            for c in range(chunks):
                nc.tensor.transpose(turned_back[i][:, c, :], zp_cols[:, c : c + 1].to_broadcast([P, P]), ident[:])

        for i in range(pieces - 1):
            turn_back(i, keep.tile([P, ZP_PIECES[i] // P], F32, name=f"zp_cols{i}"))

        w_grouped = shared.tile([P, N, PACK], BF16, name="w_grouped", align_bytes=64, offset=AT_ROUNDED)
        nc.scalar.copy(
            out=w_grouped[:].rearrange("p (c i) t -> p c t i", i=PACK),
            in_=w_raw[:].rearrange("p t (c i) -> p c t i", i=PACK),
        )
        turn_back(pieces - 1, shared.tile([P, 1], F32, name="late_col", align_bytes=64, offset=AT_LATE_COL))
        zp_spread = shared.tile([P, S], F32, name="zp_spread", align_bytes=64, offset=AT_SPREAD)
        for i, back in enumerate(turned_back):
            nc.scalar.copy(out=zp_spread[:, starts[i] : starts[i + 1]], in_=back[:].rearrange("p c n -> p (c n)"))

        nc.vector.tensor_copy(out=word_table[:, 0:EARLY_WORDS], in_=early_words[:])
        first_codes = keep.tile([P, FIRST], U32, name="first_codes", align_bytes=64)
        nc.vector.tensor_copy(out=first_codes[:], in_=word_table[:].bitcast(U32).indirect(offsets[:, 0 : FIRST // GROUP]))
        w_codes = keep.tile([P, N], U32, name="w_codes", align_bytes=64)
        w_scale = keep.tile([P, N], U8, name="w_scale", align_bytes=64)
        nc.vector.quantize_mx(
            out=w_codes[:].bitcast(FP8X4), scales=w_scale[:], in_=w_grouped[:].rearrange("p n j -> p (n j)")
        )
        second_codes = shared.tile([P, SECOND], U32, name="second_codes", align_bytes=64, offset=AT_SECOND_CODES)
        nc.vector.tensor_copy(out=second_codes[:], in_=word_table[:].bitcast(U32).indirect(offsets[:, FIRST // GROUP :]))
        x_codes = [first_codes, second_codes]

        negated = keep.tile([P, S], F32, name="negated", align_bytes=64)
        result = keep.tile([P, S], F32, name="result", align_bytes=64)
        for first, width, b in PRODUCTS:
            h, in_half = (0, first) if first < FIRST else (1, first - FIRST)
            acc = psum.tile([P, width], F32, name=f"acc{first}", tag=f"bank{b}")
            nc.tensor.matmul_mx(
                out=acc[:],
                lhsT=w_codes[:].bitcast(FP8X4),
                lhsT_scale=w_scale[:],
                rhs=x_codes[h][:, in_half : in_half + width].bitcast(FP8X4),
                rhs_scale=x_scale[:, first : first + width],
                start=True,
                stop=True,
            )
            for at in range(0, width, FINISH_WIDTH):
                cols = slice(first + at, first + at + FINISH_WIDTH)
                nc.vector.scalar_tensor_tensor(
                    out=negated[:, cols],
                    in0=zp_spread[:, cols],
                    scalar=csum_col[:],
                    in1=acc[:, at : at + FINISH_WIDTH],
                    op0=ALU.mult,
                    op1=ALU.subtract,
                )
                nc.scalar.activation(out=result[:, cols], in_=negated[:, cols], func=ACT.Gelu_apprx_tanh, scale=-1.0)
        for first, width in STORES:
            nc.sync.dma_start(out=out[:, first : first + width], in_=result[:, first : first + width])
